import numpy as np, ml_dtypes
CORES = [13,21,141,149]
N = 4
BF = ml_dtypes.bfloat16
def gentries(a):
    return np.ascontiguousarray(a.reshape(8, 16, -1).transpose(0, 2, 1)).reshape(8, -1)
def gtable(e):
    e = np.asarray(e); return np.ascontiguousarray(e.reshape(8, -1, 16).transpose(0, 2, 1)).reshape(128, -1).astype(np.int32)
W, K, E, X, S, RO = 4096, 1536, 96, 2, 4, 2
ANY = np.arange(256); LEN = np.arange(1, 13)
def place(u1, u2, m):
    return ((((u1 & 4095) * (u2 & 4095)) >> 5) + u2 + 97 * m) & (W - 1)
def hashes(st, m, wt):
    u = np.where(np.arange(12) < m[:, None], st, 0) @ wt
    return place(u[:, 0], u[:, 1], m)
def ropes(rng, shape, lens):
    n = np.minimum(rng.integers(0, 8, shape), 4)
    return np.where(np.arange(4) < n[..., None], lens[rng.integers(0, len(lens), shape + (4,))], 0)
def fill(rng):
    return np.concatenate([rng.integers(0, 256, (N, 8, 12, W)), np.moveaxis(ropes(rng, (N, 8, W), LEN), 3, 2)], axis=2)
def pool(rng, M, vals):
    st = vals[rng.integers(0, len(vals), (M, 12))]; h = max(M // 8, 1); keep = rng.integers(0, 13, M); keep[:h] = 0
    return np.where(np.arange(12) < keep[:, None], st[rng.integers(0, h, M)], st)
def plant(T, st, m, ro, wt):
    h = hashes(st, m, wt); T[:, h] = np.concatenate([st.T, ro.T])
def asks(rng, st, vals, lens):
    x = st[rng.integers(0, len(st), K)]; cut = np.where(rng.random(K) < 0.3, rng.integers(0, 13, K), 12)
    x = np.where(np.arange(12) < cut[:, None], x, vals[rng.integers(0, len(vals), (K, 12))])
    return np.concatenate([x.T, ropes(rng, (K,), lens).T])
def parts(rng, wt, M, n, vals, lens):
    P = fill(rng); q = np.zeros((N, 8, 16, K), np.int64)
    for g in range(8):
        st = pool(rng, int(M[g]), vals)
        for a in range(N):
            plant(P[a, g], st[rng.integers(0, len(st), n)], lens[rng.integers(0, len(lens), n)], ropes(rng, (n,), lens), wt[a, g])
            q[a, g] = asks(rng, st, vals, lens)
    return P, q
def alike_ropes(n, l):
    return np.tile(np.array((tuple(l) + (0, 0, 0, 0))[:4]), (n, 1))
def steer(rng, c):
    v = ((np.diff(c, axis=1, prepend=0) - 194) & (W - 1)) + W * rng.integers(0, 65280 // W, c.shape)
    return np.stack([v % 255, v // 255], axis=2).reshape(len(c), 12)
def meetings(rng, ends):
    n = 6; F = 2 + 2 * S; cut = 2 + n * np.arange(7); four = (6, 8, 10, 12)
    c = 1 + rng.permutation(W - 2)[:(2 + 7 * n) * 6].reshape(-1, 6)
    d, s1, e1, q2, s3, o3, q4, s5 = np.split(c, cut)
    for i in range(2): d[i, ends[i][0]] = ends[i][1]
    s1[:, 1] = s1[:, 0]; e1[:, 0] = s1[:, 0]
    q2[:, S] = q2[:, 1]
    s3[:, S - 1] = s3[:, S]; o3[:, :2] = s3[:, :2]
    q4[:, 3] = q4[:, 1]
    s5[:, 5] = s5[:, 2]
    x = steer(rng, c); d, s1, e1, q2, s3, o3, q4, s5 = np.split(x, cut)
    e1[:, :2] = s1[:, :2]; o3[:, :4] = s3[:, :4]
    r2 = q2.copy(); r2[:, 4:] = (r2[:, 4:] + rng.integers(1, 256, (n, 8))) & 255
    r4 = q4.copy(); r4[:, 4:] = (r4[:, 4:] + rng.integers(1, 256, (n, 8))) & 255
    marks = [(d, 4, four), (d, F + 2, ()), (s1, 4, four), (s1, F + 2, ()), (r2, 4, four), (q2, F + 2, ()), (s3, 4, four), (s3, F + 2, ()), (o3, F, ()), (r4, 4, ()), (s5, 4, (6,))]
    ask = [(d, (4,)), (s1, (4,)), (q2, (F,)), (s3, (4,)), (o3, (4,)), (q4, (8,)), (s5, (4,)), (s5, (12,)), (e1, (12, 2)), (q2, (4,)), (q4, (8, 4))]
    return marks, np.concatenate([y for y, l in ask]), np.concatenate([alike_ropes(len(y), l) for y, l in ask]), 2 + 7 * n
def pack(P, q, wt):
    w = np.concatenate([wt, np.zeros((N, 8, 4, 2), np.int64)], axis=2)
    return {"mk": P.reshape(N, 128, W).astype(np.float32).astype(BF), "qs": q.reshape(N, 128, K).astype(np.float32).astype(BF), "wt": w.reshape(N, 128, 2).astype(np.float32).astype(BF)}
def setup_inputs(rng):
    wt = rng.integers(0, 256, (N, 8, 12, 2)); P, q = parts(rng, wt, [512] * 8, 3 * W // 4, ANY, LEN)
    return pack(P, q, wt)
def setup_inputs_alike(rng):
    wt = rng.integers(0, 256, (N, 8, 12, 2)); P, q = parts(rng, wt, rng.integers(16, 33, 8), 160, ANY, LEN)
    return pack(P, q, wt)
def setup_inputs_ends(rng):
    wt = rng.choice(np.array([0, 1, 255]), (N, 8, 12, 2)); wt[:, 3] = 0; wt[:, 5] = 255
    for g in (0, 1, 6):
        wt[:, g] = 0; wt[:, g, 0::2, 1] = 1; wt[:, g, 1::2, 1] = 255
    P, q = parts(rng, wt, [64] * 8, W // 4, np.array([0, 255, 0, 1, 254]), np.array([1, 12, 1, 12, 2, 11]))
    for g, ends in ((0, ((S, 0), (1, W - 1))), (1, ((S + 1, 0), (S + 1, W - 1))), (6, ((S, W - 1), (1, 0)))):
        marks, st, ro, look = meetings(rng, ends)
        for a in range(N):
            for y, m, l in marks: plant(P[a, g], y, np.full(len(y), m), alike_ropes(len(y), l), wt[a, g])
            j = np.concatenate([rng.permutation(len(st)), rng.integers(0, look, K - len(st))])
            q[a, g] = np.concatenate([st[j].T, ro[j].T])
    x = rng.integers(225, 256, (2048, 12)); x = x[np.unique(np.sum(x, axis=1), return_index=True)[1]]
    u = 255 * np.sum(x, axis=1); x = x[np.argsort(-((((u & 4095) ** 2) >> 5) + u))[:24]]
    for a in range(N):
        plant(P[a, 5], x, np.full(len(x), 12), np.zeros((len(x), 4), np.int64), wt[a, 5])
        t = rng.permutation(K)[:96]; q[a, 5][:12, t] = x[np.arange(96) % len(x)].T; q[a, 5][12:, t] = np.array([12, 0, 0, 0])[:, None]
    return pack(P, q, wt)
def setup_inputs_full(rng):
    w = rng.integers(0, 256, (8, 12, 2)); wt = np.stack([w] * N); P = fill(rng); q = np.zeros((N, 8, 16, K), np.int64)
    for g in range(8):
        st = rng.integers(0, 256, (2048, 12)); hs = np.stack([hashes(st, np.full(2048, m), w[g]) for m in [5] + [9 + i for i in range(S)]])
        used = set(); keep = []
        for i in range(2048):
            c = set(hs[:, i].tolist())
            if len(keep) < E and len(c) == S + 1 and not (c & used):
                used |= c; keep.append(i)
        x = st[np.array(keep)]; n = len(keep)
        for a in range(N):
            plant(P[a, g], x, np.full(n, 5), np.stack([np.array([9, 10, 11, 12])] * n), w[g])
            plant(P[a, g], x, np.full(n, 8 + S), np.zeros((n, 4), np.int64), w[g])
            j = np.concatenate([rng.permutation(n), rng.integers(0, n, K - n)])
            first = (rng.random(K) < 0.5) | (np.arange(K) < n)
            ro = np.where(first[:, None], np.array([5, 8, 0, 0]), np.array([7 + S, 5, 12, 0]))
            q[a, g] = np.concatenate([x[j].T, ro.T])
    return pack(P, q, wt)
def setup_inputs_still(rng):
    wt = rng.integers(0, 256, (N, 8, 12, 2)); P, q = parts(rng, wt, [256] * 8, W // 2, ANY, LEN); e = rng.permutation(8)
    q[:, :, 12:] = np.where(rng.random((N, 8, 1, K)) < 0.5, 0, q[:, :, 12:])
    q[:, e[0], 12:] = 0; P[:, e[1], 12:] = 0; q[:, e[2], :12] = rng.integers(0, 256, (N, 12, K))
    q[:, e[2], 12:] = np.where(q[:, e[2], 12:] > 0, np.maximum(q[:, e[2], 12:], 4), 0)
    return pack(P, q, wt)
def setup_inputs_spread(rng):
    vals = np.minimum(np.exp2(8.01 * rng.random(512)).astype(np.int64), 256) - 1
    wt = vals[rng.integers(0, 512, (N, 8, 12, 2))]; P, q = parts(rng, wt, 2 ** rng.integers(3, 12, 8), W // 2, vals, LEN)
    return pack(P, q, wt)
def check_inputs(d):
    bad = []
    for k, n in (("mk", W), ("qs", K), ("wt", 2)):
        v = np.asarray(d[k]).astype(np.float32).reshape(N, 8, 16, n)
        if not np.all(v == np.floor(v)): bad.append("whole numbers of " + k)
        if not (np.min(v) >= 0 and np.max(v[:, :, :12]) <= 255): bad.append("range of " + k)
        if not np.max(v[:, :, 12:]) <= (0 if k == "wt" else 12): bad.append("last four rows of " + k)
        if k != "wt" and np.any((v[:, :, 12:15] == 0) & (v[:, :, 13:] > 0)): bad.append("ropes of " + k)
    return bad
def reference(mk, qs, wt):
    P = mk.astype(np.float32).astype(np.int32).reshape(N, 8, 16, W); q = qs.astype(np.float32).astype(np.int32).reshape(N, 8, 16, K)
    w = np.ascontiguousarray(wt.astype(np.float32).astype(np.int32).reshape(N, 8, 16, 2)[:, :, :12].transpose(0, 1, 3, 2))
    p = np.arange(12, dtype=np.int32)[:, None]
    for rnd in range(RO):
        sy = q[:, :, :12]; ro = q[:, :, 12:]
        b = np.full((N, 8, K), -1, np.int32); f = np.full((N, 8, K), -1, np.int32); mb = np.zeros((N, 8, K), np.int32); mf = np.zeros((N, 8, K), np.int32)
        for step in range(S):
            m = ro[:, :, 0]
            u = np.matmul(w, np.where(p < m[:, :, None], sy, 0))
            h = place(u[:, :, 0], u[:, :, 1], m)
            v = np.take_along_axis(P, h[:, :, None], axis=3)
            same = np.all((v[:, :, :12] == sy) | (p >= m[:, :, None]), axis=2)
            hit = (m > 0) & same; miss = (m > 0) & ~same
            b = np.where(hit, h, b); mb = np.where(hit, m, mb)
            f = np.where(miss, h, np.where(hit, -1, f)); mf = np.where(miss, m, mf)
            less = np.concatenate([ro[:, :, 1:], np.zeros((N, 8, 1, K), np.int32)], axis=2)
            ro = np.where(hit[:, :, None], v[:, :, 12:], np.where(miss[:, :, None], less, ro))
        old = np.take_along_axis(P, np.maximum(b, 0)[:, :, None], axis=3)[:, :, :12]
        new = q.copy(); new[:, :, :12] = np.where((b >= 0)[:, :, None] & (p < mb[:, :, None] + X), old, sy)
        if rnd < RO - 1:
            for a in range(N):
                for g in range(8):
                    T = P[a, g]; c = np.nonzero((b[a, g, :E] >= 0) & (f[a, g, :E] >= 0))[0]
                    t = c[np.unique(f[a, g, c], return_index=True)[1]]
                    T[:, f[a, g, t]] = np.concatenate([sy[a, g][:, t], ro[a, g][:, t]])
                    t = c[np.unique(b[a, g, c], return_index=True)[1]]
                    have = T[12:15, b[a, g, t]]
                    T[12:, b[a, g, t]] = np.concatenate([mf[a, g, t][None], have])
            q = np.ascontiguousarray(new.reshape(N, 8, 16, N, K // N).transpose(3, 1, 2, 0, 4)).reshape(N, 8, 16, K)
    return {"yq": new.reshape(N, 128, K).astype(np.float32).astype(BF), "yb": np.stack([gtable(x) for x in b]).astype(np.float32)}

@@ -1,0 +1,642 @@
+from concourse.mybir import AluOpType as Op, ActivationFunctionType as Fn, AxisListType
+
+W, K, NB = 4096, 1536, 384
+CH, NJ = 768, 48
+MKW = W + 128
+LN256 = 5.545177444479562
+
+_sets = ["LX", "LY", "LN", "LV0", "LV1", "LV2", "LV3", "LB", "BIG"]
+_mats = ["JR", "JA", "JP", "BD", "ID", "HI", "NI", "R0", "ISY", "SRC", "CAQ", "CA", "RS", "DN", "R12"]
+SCRATCH = {"mkT": ("sbuf", [128, MKW], "bfloat16"), "land": ("sbuf", [128, NB], "bfloat16")}
+for _n in ("qN", "qA", "qB", "qF", "zz", "nn", "vv", "dd", "sd"):
+    SCRATCH[_n] = ("sbuf", [128, K], "bfloat16")
+for _n in ("qj", "zp"):
+    SCRATCH[_n] = ("sbuf", [128, K], "float32")
+for _n in _sets:
+    SCRATCH[_n] = ("sbuf", [128, 2048], "bfloat16")
+for _n in _mats:
+    SCRATCH[_n] = ("sbuf", [128, 128], "bfloat16")
+
+
+def _add(dtype, **widths):
+    for n, w in widths.items():
+        SCRATCH[n] = ("sbuf", [128, w], dtype)
+
+
+_add("bfloat16", wS=2, Aw=384, tm=288, Lb=96, khb=32, sb=16, cm=96, Eb=96, vb=96, mf=96, Sb=96)
+_add("int32", pi=1, ki=1, ci=4, U=192, UA=192, P=96, Kk=96, Wd=96, S=96, H=96, codeS=384, ch=96, B=96, Hb=96, Li=96,
+     fc=192, f1=32, FB=12, cl=12, key=12, kh=24, si=16)
+_add("float32", col=32, E256=16, geo=64, IT=96, LM=576, DU=12, hitS=384, th=96, m97=96, mt=192, y1=96, y2=96, y3=96, yS=96,
+     al=192, ms=192, ed=32, ed2=12, nk=12, key1=12, LK=1152, EQ=1152, CNT=12, w1=64, mk1=96)
+_add("uint16", OFF=96, OB=96, OE=12)
+BANKS = ("g00", "g01", "g10", "g11", "h0", "h1", "k0", "k1")
+for _n in BANKS:
+    SCRATCH[_n] = ("psum", [128, 512], "float32")
+SEMAPHORES = ["sV", "sA", "sP", "sG", "dw", "dq0", "dq1", "dm0", "dm1", "dy0", "dy1", "dyb",
+              "arr0", "arr1", "arr2", "arr3", "sent", "rin", "rls"]
+
+
+def relay_of(src, dst, cores, topo):
+    k = 0
+    for d in cores:
+        if d == src or topo.may_write(src, d):
+            if d == dst:
+                return None
+            continue
+        own = [c for c in topo.cores_of(src) if c != src and topo.may_write(c, d)]
+        near = [c for c in own if topo.die(c) == topo.die(src)]
+        far = [c for c in own if topo.die(c) != topo.die(src)]
+        if d == dst:
+            return near[0] if k % 2 == 0 else far[0]
+        k += 1
+    return None
+
+
+def count(mask):
+    return bin(mask).count("1")
+
+
+def off_chip_mask(src, cores, topo):
+    for d in cores:
+        if d != src and topo.may_write(src, d):
+            return topo.mask(src, d)
+    return 0
+
+
+def rank_program(g, core, T, topo):
+    cores = list(T.cores)
+    rank = T.rank_of(core)
+    if rank is None:
+        for a in cores:
+            for b in cores:
+                if a == b or relay_of(a, b, cores, topo) != core:
+                    continue
+                r = T.rank_of(a)
+                m_in = off_chip_mask(a, cores, topo) & topo.mask(a, core)
+                m_out = topo.mask(core, b)
+                rid, pid = topo.addr(b, core)
+                g.wait_ge(T.sem.rin, count(m_in))
+                g.remote_dma(T.qB[:, NB * r:NB * r + NB], T.land[:], T.sem["arr%d" % r], T.sem.rls, pid, rid, m_out)
+                g.wait_ge(T.sem.rls, count(m_out))
+        return
+
+    Q = {"v": g.vector, "a": g.scalar, "p": g.tensor, "g": g, "s": g.sync}
+    SEM = {"v": "sV", "a": "sA", "p": "sP", "g": "sG"}
+    cnt = {"v": 0, "a": 0, "p": 0, "g": 0}
+    clock = {q: {} for q in Q}
+    clkat = {}
+    rec = {}
+    bank = {}
+    total = {}
+
+    def see(q, ev):
+        c = clock[q]
+        for s, x in clkat.get(ev, {}).items():
+            if c.get(s, 0) < x:
+                c[s] = x
+        if c.get(ev[0], 0) < ev[1]:
+            c[ev[0]] = ev[1]
+
+    def await_all(q, evs):
+        best = {}
+        for s, x in evs:
+            best[s] = max(best.get(s, 0), x)
+        todo = [(s, x) for s, x in best.items() if clock[q].get(s, 0) < x]
+        keep = []
+        for e in todo:
+            if not any(o != e and clkat.get(o, {}).get(e[0], 0) >= e[1] for o in todo):
+                keep.append(e)
+        for s, x in keep:
+            Q[q].wait_ge(T.sem[s], x)
+            see(q, (s, x))
+
+    def conflicts(q, reads, writes, dma):
+        evs = []
+        for kind, lst in (("r", reads), ("w", writes)):
+            for b in lst:
+                nm, lo, hi = b[0], b[1], b[2]
+                if nm in BANKS:
+                    for q2, st in bank.get(nm, {}).items():
+                        if q2 != q:
+                            evs.append(st[0])
+                        elif q != "p" and st[1] is not None:
+                            evs.append(st[1])
+                    continue
+                for l2, h2, q2, ev, k2 in rec.get(nm, ()):
+                    if l2 < hi and lo < h2 and (kind == "w" or k2 == "w"):
+                        if k2 == "r" and q2 == q and not dma:
+                            continue
+                        evs.append(ev)
+        return evs
+
+    def note(q, reads, writes, ev, dma):
+        qn = "dma" if dma else q
+        for b in reads:
+            if b[0] in BANKS:
+                st = bank.setdefault(b[0], {}).get(q, (None, None))
+                bank[b[0]][q] = (ev, st[1])
+            else:
+                lst = rec.setdefault(b[0], [])
+                lst[:] = [x for x in lst if not (x[4] == "r" and x[2] == qn and not dma and b[1] <= x[0] and x[1] <= b[2])]
+                lst.append((b[1], b[2], qn, ev, "r"))
+        for b in writes:
+            if b[0] in BANKS:
+                bank.setdefault(b[0], {})[q] = (ev, ev)
+            else:
+                lst = rec.setdefault(b[0], [])
+                lst[:] = [x for x in lst if not (b[1] <= x[0] and x[1] <= b[2])]
+                lst.append((b[1], b[2], qn, ev, "w"))
+
+    def emit(q, fn, reads, writes, sem=None):
+        await_all(q, conflicts(q, reads, writes, sem is not None))
+        ins = fn()
+        if sem is None:
+            cnt[q] += 1
+            ev = (SEM[q], cnt[q])
+            ins.then_inc(T.sem[SEM[q]], 1)
+        else:
+            ev = (sem, 16)
+            ins.then_inc(T.sem[sem], 16)
+        total[ev[0]] = ev[1]
+        c = dict(clock[q])
+        c[ev[0]] = ev[1]
+        clkat[ev] = c
+        note(q, reads, writes, ev, sem is not None)
+        return ev
+
+    def ap(b):
+        if len(b) > 3:
+            return T[b[0]][:, b[1]:b[2]:b[3]]
+        return T[b[0]][:, b[1]:b[2]]
+
+    def isap(x):
+        return isinstance(x, tuple)
+
+    def tt(out, a, b, op):
+        return emit("v", lambda: g.vector.tensor_tensor(ap(out), ap(a), ap(b), op), [a, b], [out])
+
+    def ts(out, a, s1, op0, s2=None, op1=None):
+        rd = [a] + [s for s in (s1, s2) if isap(s)]
+        x1 = ap(s1) if isap(s1) else s1
+        x2 = ap(s2) if isap(s2) else s2
+        if op1 is None:
+            return emit("v", lambda: g.vector.tensor_scalar(ap(out), ap(a), x1, None, op0), rd, [out])
+        return emit("v", lambda: g.vector.tensor_scalar(ap(out), ap(a), x1, x2, op0, op1), rd, [out])
+
+    def cp(out, a):
+        return emit("v", lambda: g.vector.tensor_copy(ap(out), ap(a)), [a], [out])
+
+    def fill(out, x):
+        return emit("v", lambda: g.vector.memset(ap(out), x), [], [out])
+
+    def act(out, a, fn, bias=0.0, scale=1.0, accum=None):
+        rd = [a] + [s for s in (bias, scale) if isap(s)]
+        kw = {}
+        if isap(bias) or bias != 0.0:
+            kw["bias"] = ap(bias) if isap(bias) else bias
+        if isap(scale) or scale != 1.0:
+            kw["scale"] = ap(scale) if isap(scale) else scale
+        wr = [out]
+        if accum is not None:
+            kw["accum_out"] = ap(accum)
+            wr = [out, accum]
+        return emit("a", lambda: g.scalar.activation(ap(out), ap(a), fn, **kw), rd, wr)
+
+    def mm(seq, reads, writes):
+        def go():
+            ins = None
+            for o, l, r, st, sp in seq:
+                ins = g.tensor.matmul(ap(o), ap(l), ap(r), st, sp)
+            return ins
+        return emit("p", go, reads, writes)
+
+    def LJ(nm, j):
+        return (nm, 128 * j, 128 * j + 128)
+
+    def M(nm):
+        return (nm, 0, 128)
+
+    def word(nm, out, src, base, w, extra=None, strided=True):
+        seq = []
+        if extra is not None:
+            seq.append((out, extra[0], extra[1], True, False))
+        for j in range(16):
+            r = (src, base + j, base + 16 * w, 16) if strided else (src, base + w * j, base + w * (j + 1))
+            seq.append((out, LJ(nm, j), r, extra is None and j == 0, j == 15))
+        rd = [(nm, 0, 2048), (src, base, base + 16 * w)]
+        if extra is not None:
+            rd += [extra[0], extra[1]]
+        return mm(seq, rd, [out])
+
+    emit("a", lambda: g.scalar.dma_start(ap(("wS", 0, 2)), T.wt[:]), [], [("wS", 0, 2)], "dw")
+    for c in range(2):
+        emit("s", lambda: g.sync.dma_start(ap(("qN", CH * c, CH * c + CH)), T.qs[:, CH * c:CH * c + CH]), [],
+             [("qN", CH * c, CH * c + CH)], "dq%d" % c)
+    emit("a", lambda: g.scalar.dma_start(ap(("mkT", 0, 2048)), T.mk[:, 0:2048]), [], [("mkT", 0, 2048)], "dm0")
+    emit("s", lambda: g.sync.dma_start(ap(("mkT", 2048, W)), T.mk[:, 2048:W]), [], [("mkT", 2048, W)], "dm1")
+
+    def C(i):
+        return ("col", i, i + 1)
+    KC, PB, NBI, LBI, WN, KP1, RCOL, KK, T0, T1, R120 = [C(i) for i in range(11)]
+    RC = [C(12 + r) for r in range(4)]
+    KJ = [C(16 + J) for J in range(6)]
+    KLT = C(22)
+
+    def iota(out, pattern, base, cm, flag=True):
+        if flag:
+            return emit("g", lambda: g.iota(ap(out), pattern, base, cm, allow_small_or_imprecise_dtypes=True), [], [out])
+        return emit("g", lambda: g.iota(ap(out), pattern, base, cm), [], [out])
+
+    def pick(out, a, pattern, op, x, base, cm):
+        return emit("g", lambda: g.affine_select(ap(out), ap(a), pattern, op, x, base, cm), [a], [out])
+
+    iota(("pi", 0, 1), [[0, 1]], 0, 1, False)
+    iota(M("JR"), [[0, 8], [1, 16]], 0, 0)
+    pick(M("JA"), M("JR"), [[-16, 8], [0, 16]], Op.is_ge, 99.0, 0, 1)
+    pick(M("JP"), M("JA"), [[16, 8], [0, 16]], Op.is_ge, 99.0, 15, -1)
+    ts(("ki", 0, 1), ("pi", 0, 1), 15, Op.bitwise_and)
+    cp(KC, ("ki", 0, 1))
+    ts(PB, KC, 256.0, Op.mult)
+    ts(NBI, KC, -256.0, Op.mult)
+    for r in range(4):
+        ts(RC[r], KC, float(12 + r), Op.is_equal)
+    ts(M("ID"), M("JP"), KC, Op.is_equal)
+    ts(M("BD"), M("JP"), 15.5, Op.is_le)
+    ts(M("R0"), M("BD"), RC[0], Op.mult, 256.0, Op.mult)
+    for j in range(16):
+        ts(LJ("BIG", j), M("JP"), float(j), Op.is_equal)
+
+    def full(nm):
+        return (nm, 0, 2048)
+    ts(full("LX"), full("BIG"), ("wS", 0, 1), Op.mult)
+    ts(full("LY"), full("BIG"), ("wS", 1, 2), Op.mult)
+    act(full("LV0"), full("BIG"), Fn.Copy, scale=RC[0])
+    pick(full("LV1"), full("BIG"), [[0, 16], [-16, 8], [0, 16]], Op.is_equal, 0.0, -13, 1)
+    iota(M("SRC"), [[0, 8], [1, 4], [1, 4]], 13, 0)
+    iota(("IT", 0, 96), [[1, 96]], 0, 0)
+    iota(("w1", 0, 12), [[0, 2], [16, 6]], W, 0)
+
+    def consts_search():
+        ts(("E256", 0, 16), ("JR", 0, 16), KC, Op.is_equal, 256.0, Op.mult)
+        fill(("geo", 0, 16), 1.0 / 256)
+        fill(("geo", 16, 32), 0.0)
+        emit("v", lambda: g.vector.tensor_tensor_scan(ap(("geo", 32, 48)), ap(("geo", 0, 16)), ap(("geo", 16, 32)), -128.0,
+                                                      Op.mult, Op.add), [("geo", 0, 32)], [("geo", 32, 48)])
+        tt(("geo", 48, 60), ("geo", 32, 44), ("E256", 0, 12), Op.mult)
+        emit("v", lambda: g.vector.tensor_reduce(ap(WN), ap(("geo", 48, 60)), AxisListType.X, Op.add), [("geo", 48, 60)], [WN])
+        ts(full("LN"), full("BIG"), WN, Op.mult, 1.0 / 256, Op.mult)
+        ts(full("LV2"), full("BIG"), RC[2], Op.mult)
+        ts(full("LV3"), full("BIG"), RC[3], Op.mult)
+        ts(M("NI"), M("ID"), -1.0, Op.mult)
+
+    def consts_bcast():
+        for j in range(16):
+            ts(LJ("LB", j), M("BD"), ("E256", j, j + 1), Op.mult)
+
+    def consts_late():
+        ts(M("HI"), M("ID"), 0.5, Op.mult)
+        ts(T0, KC, 11.5, Op.is_gt, -100000.0, Op.mult)
+        ts(T1, NBI, 128.0, Op.subtract)
+        tt(LBI, T0, T1, Op.add)
+        fill(("mkT", W, MKW), 0.0)
+
+    def consts_edits():
+        ts(KLT, KC, 11.5, Op.is_lt)
+        ts(M("ISY"), M("ID"), KLT, Op.mult)
+        ts(M("CAQ"), M("SRC"), KC, Op.is_equal)
+        tt(M("CA"), M("CAQ"), M("BD"), Op.mult)
+        ts(("ci", 0, 1), ("ki", 0, 1), 3, Op.bitwise_and)
+        ts(T0, KC, 11.5, Op.is_gt, 50.0, Op.mult)
+        ts(T1, ("ci", 0, 1), 12.0, Op.add)
+        tt(RCOL, T0, T1, Op.add)
+        ts(M("RS"), M("JP"), RCOL, Op.is_equal)
+        ts(("ci", 1, 2), ("ki", 0, 1), 2, Op.arith_shift_right)
+        ts(KK, ("ci", 1, 2), -256.0, Op.mult, 768.0, Op.add)
+        ts(T0, KC, 11.5, Op.is_lt, 50.0, Op.mult)
+        ts(T1, KC, 1.0, Op.add)
+        tt(KP1, T0, T1, Op.add)
+        ts(M("DN"), M("JP"), KP1, Op.is_equal)
+        ts(R120, RC[0], 1.0 / 256, Op.mult)
+        ts(M("R12"), M("ID"), R120, Op.mult)
+        ts(("DU", 0, 12), ("w1", 0, 12), KC, Op.add)
+        for J in range(6):
+            ts(KJ[J], KC, 16.0 * J, Op.add)
+            ts(("LM", 96 * J, 96 * J + 96), ("IT", 0, 96), KJ[J], Op.is_lt)
+
+    def sm(nm, c, k=0, n=1):
+        lo = c * NJ * n + k * NJ
+        return (nm, lo, lo + NJ)
+
+    def half(nm, c, h):
+        lo = c * CH + h * 384
+        return (nm, lo, lo + 384)
+
+    def chunk(nm, c):
+        return (nm, c * CH, c * CH + CH)
+
+    def gb(c, h):
+        return "g%d%d" % (c, h)
+
+    def jmajor(c, src):
+        for h, bk in ((0, "h%d" % c), (1, "k%d" % c)):
+            seq = []
+            for x in range(8):
+                seq.append(((bk, x * NJ, x * NJ + NJ), M("ID"), (src, c * CH + 8 * h + x, c * CH + CH, 16), True, True))
+            mm(seq, [M("ID"), chunk(src, c)], [(bk, 0, 384)])
+            act(half("qj", c, h), (bk, 0, 384), Fn.Identity, bias=PB)
+
+    def lengths(c, src, rs):
+        for r in rs:
+            word("LV%d" % r, ("k%d" % c, r * NJ, r * NJ + NJ), src, c * CH, NJ)
+        lo, hi = rs[0] * NJ, rs[-1] * NJ + NJ
+        act(("Aw", c * 192 + lo, c * 192 + hi), ("k%d" % c, lo, hi), Fn.Copy)
+
+    def P1(c, s, src):
+        m = sm("Aw", c, s - 1, 4)
+        for h in range(2):
+            seq = []
+            for x in range(8):
+                j = 8 * h + x
+                o = (gb(c, h), x * NJ, x * NJ + NJ)
+                if s == 1:
+                    seq.append((o, M("R0"), (src, c * CH + j, c * CH + CH, 16), True, True))
+                else:
+                    seq.append((o, LJ("LB", j), m, True, True))
+            mm(seq, [M("R0"), chunk(src, c)] if s == 1 else [full("LB"), m], [(gb(c, h), 0, 384)])
+
+    def V1(c):
+        for h in range(2):
+            tt(half("zp", c, h), half("qj", c, h), (gb(c, h), 0, 384), Op.min)
+
+    def A1(c):
+        for h in range(2):
+            act(half("zz", c, h), half("zp", c, h), Fn.Relu, bias=NBI)
+
+    def A2(c, s):
+        m = sm("Aw", c, s - 1, 4)
+        act(sm("m97", c), m, Fn.Copy, scale=97.0)
+        act(sm("th", c), m, Fn.Silu, scale=-LN256)
+        act(sm("mt", c, s % 2, 2), m, Fn.Copy, bias=8192.0 + 65536.0 * s, scale=4096.0)
+
+    def P2(c):
+        word("LX", ("h%d" % c, 0, NJ), "zz", c * CH, NJ, strided=False)
+        word("LY", ("h%d" % c, NJ, 2 * NJ), "zz", c * CH, NJ, strided=False)
+
+    def V2(c):
+        hb = "h%d" % c
+        u = ("U", c * 96, c * 96 + 96)
+        ua = ("UA", c * 96, c * 96 + 96)
+        return [lambda: cp(u, (hb, 0, 96)),
+                lambda: tt(sm("Wd", c), (hb, NJ, 96), sm("m97", c), Op.add),
+                lambda: ts(ua, u, 4095, Op.bitwise_and),
+                lambda: tt(sm("P", c), ("UA", c * 96, c * 96 + NJ), ("UA", c * 96 + NJ, c * 96 + 96), Op.mult),
+                lambda: ts(sm("Kk", c), sm("P", c), 5, Op.arith_shift_right),
+                lambda: tt(sm("S", c), sm("Kk", c), sm("Wd", c), Op.add),
+                lambda: ts(sm("H", c), sm("S", c), 4095, Op.bitwise_and),
+                lambda: cp(sm("OFF", c), sm("H", c))]
+
+    def win(off, w=W):
+        return T.mkT[:, 0:w].indirect(ap(off))
+
+    def V3(c, src):
+        o, off, q = chunk("nn", c), sm("OFF", c), chunk(src, c)
+        emit("v", lambda: g.vector.tensor_tensor(ap(o), win(off), ap(q), Op.not_equal), [("mkT", 0, W), off, q], [o])
+
+    def A3(c):
+        o, off = chunk("vv", c), sm("OFF", c)
+        emit("a", lambda: g.scalar.activation(ap(o), win(off), Fn.Copy), [("mkT", 0, W), off], [o])
+
+    def P3(c):
+        word("LN", ("k%d" % c, 0, NJ), "nn", c * CH, NJ)
+
+    def held(c, w):
+        return ("k%d" % c, NJ, 2 * NJ) if w == 0 else ("h%d" % c, (w - 1) * NJ, w * NJ)
+
+    def P4(c, s):
+        for w in range(4 - s):
+            word("LV%d" % w, held(c, w), "vv", c * CH, NJ, extra=(M("NI"), sm("Aw", c, s + w, 4)))
+
+    def tail(c, s):
+        hit, code = sm("hitS", c, s - 1, 4), sm("codeS", c, s - 1, 4)
+        first = [lambda: tt(hit, ("k%d" % c, 0, NJ), sm("th", c), Op.is_gt),
+                 lambda: tt(code, sm("H", c), sm("mt", c, s % 2, 2), Op.add)]
+        mul, add = [], []
+        for w in range(4 - s):
+            t = ("tm", c * 144 + w * NJ, c * 144 + w * NJ + NJ)
+            a = sm("Aw", c, s + w, 4)
+            mul.append(lambda o=held(c, w), t=t: tt(t, o, hit, Op.mult))
+            add.append(lambda a=a, t=t: tt(a, a, t, Op.add))
+        if s == 1:
+            mb = [lambda: tt(sm("B", c), code, hit, Op.mult)]
+        else:
+            mb = [lambda: tt(sm("ch", c), code, hit, Op.mult), lambda: tt(sm("B", c), sm("B", c), sm("ch", c), Op.max)]
+        if s < 4:
+            return first + mul[:1], mb[:1] + add[:1] + mul[1:] + add[1:], mb[1:]
+        return first, mb, []
+
+    def run(*lists):
+        for x in range(max(len(l) for l in lists)):
+            for l in lists:
+                if x < len(l):
+                    l[x]()
+
+    def La(c, src):
+        ts(sm("Li", c), sm("B", c), 12, Op.arith_shift_right, 15, Op.bitwise_and)
+        ts(sm("Hb", c), sm("B", c), 4095, Op.bitwise_and)
+        cp(sm("Lb", c), sm("Li", c))
+        cp(sm("OB", c), sm("Hb", c))
+        for h, lo, n in ((0, 0, 32), (1, 32, 16)):
+            r = ("Lb", c * NJ + lo, c * NJ + lo + n)
+            bk = (gb(c, h), 0, 16 * n)
+            mm([((gb(c, h), j, 16 * n, 16), LJ("LB", j), r, True, True) for j in range(16)], [full("LB"), r], [bk])
+            act(bk, bk, Fn.Sign, bias=LBI)
+        o, off, q = chunk("dd", c), sm("OB", c), chunk(src, c)
+        emit("v", lambda: g.vector.tensor_tensor(ap(o), win(off), ap(q), Op.subtract), [("mkT", 0, W), off, q], [o])
+
+    def Lb(c, src, dest):
+        for h, lo, hi in ((0, c * CH, c * CH + 512), (1, c * CH + 512, c * CH + CH)):
+            bk = (gb(c, h), 0, hi - lo)
+            tt(("sd", lo, hi), ("dd", lo, hi), bk, Op.mult)
+            mm([(bk, M("ID"), (src, lo, hi), True, False), (bk, M("HI"), ("dd", lo, hi), False, False),
+                (bk, M("HI"), ("sd", lo, hi), False, True)],
+               [M("ID"), M("HI"), (src, lo, hi), ("dd", lo, hi), ("sd", lo, hi)], [bk])
+            cuts = [lo] + [x for x in range(0, K, NB) if lo < x < hi] + [hi]
+            for x, y in zip(cuts[:-1], cuts[1:]):
+                act((dest(x, y), x, y), (gb(c, h), x - lo, y - lo), Fn.Copy)
+
+    def search(src, first):
+        for c in range(2):
+            jmajor(c, src)
+            P1(c, 1, src)
+            V1(c)
+            A1(c)
+        if first:
+            consts_search()
+        for c in range(2):
+            lengths(c, src, [0])
+            A2(c, 1)
+            P2(c)
+        late0 = late1 = []
+        for s in range(1, 5):
+            if s > 1:
+                V1(0)
+                A1(0)
+                f1, n1, late1 = tail(1, s - 1)
+                run(f1, late0)
+                run(n1)
+                P1(1, s, src)
+                A2(1, s)
+                P2(0)
+                V1(1)
+                A1(1)
+                P2(1)
+            else:
+                for c in range(2):
+                    lengths(c, src, [1, 2, 3])
+            run(V2(0), late1)
+            V3(0, src)
+            if s < 4:
+                A3(0)
+            P3(0)
+            P4(0, s)
+            run(V2(1))
+            if first and s == 1:
+                consts_bcast()
+                consts_late()
+            f0, n0, late0 = tail(0, s)
+            run(f0)
+            run(n0[:2])
+            if s < 4:
+                P1(0, s + 1, src)
+            V3(1, src)
+            if s < 4:
+                A3(1)
+                A2(0, s + 1)
+            P3(1)
+            P4(1, s)
+            late0 = n0[2:] + late0
+        run(late0)
+
+    def close(src, dest, after):
+        La(0, src)
+        for part in tail(1, 4):
+            if part:
+                run(part)
+        Lb(0, src, dest)
+        after(0)
+        La(1, src)
+        Lb(1, src, dest)
+        after(1)
+
+    omask = off_chip_mask(core, cores, topo)
+    nsent = [0]
+
+    def send(c):
+        todo = [s for s in (2 * c, 2 * c + 1) if s != rank]
+        todo.sort(key=lambda s: relay_of(core, cores[s], cores, topo) is None)
+        for s in todo:
+            b = ("qA", NB * s, NB * s + NB)
+            await_all("g", conflicts("g", [b], [], True))
+            rel = relay_of(core, cores[s], cores, topo)
+            to = cores[s] if rel is None else rel
+            m = omask & topo.mask(core, to)
+            rid, pid = topo.addr(to, core)
+            if rel is None:
+                g.remote_dma(T.qB[:, NB * rank:NB * rank + NB], ap(b), T.sem["arr%d" % rank], T.sem.sent, pid, rid, m)
+            else:
+                g.remote_dma(T.land[:], ap(b), T.sem.rin, T.sem.sent, pid, rid, m)
+            nsent[0] += count(m)
+
+    def arrivals():
+        for s in range(4):
+            if s != rank:
+                rel = relay_of(cores[s], core, cores, topo)
+                n = count(topo.mask(cores[s] if rel is None else rel, core))
+                ev = ("arr%d" % s, n)
+                clkat[ev] = {ev[0]: n}
+                total[ev[0]] = n
+                note("x", [], [("qB", NB * s, NB * s + NB)], ev, True)
+
+    def edits(src):
+        ts(("al", 0, 192), ("Aw", 0, 192), 0.0, Op.is_gt)
+        tt(("ms", 0, 192), ("al", 0, 192), ("hitS", 0, 192), Op.subtract)
+        tt(("fc", 0, 192), ("codeS", 0, 192), ("ms", 0, 192), Op.mult)
+        tt(("f1", 0, 6), ("fc", 0, 6), ("fc", NJ, NJ + 6), Op.max)
+        tt(("f1", 8, 14), ("fc", 2 * NJ, 2 * NJ + 6), ("fc", 3 * NJ, 3 * NJ + 6), Op.max)
+        tt(("FB", 0, 6), ("f1", 0, 6), ("f1", 8, 14), Op.max)
+        cp(("FB", 6, 12), ("B", 0, 6))
+        F, Bb = ("FB", 0, 6), ("B", 0, 6)
+        tt(("ed", 0, 6), F, Bb, Op.is_gt)
+        ts(("ed", 8, 14), Bb, 0.0, Op.is_gt)
+        ts(("cl", 0, 12), ("FB", 0, 12), 4095, Op.bitwise_and)
+        ts(("si", 0, 6), F, 12, Op.arith_shift_right, 15, Op.bitwise_and)
+        ts(("si", 8, 14), Bb, 16, Op.arith_shift_right)
+        for o in (0, 6):
+            tt(("ed2", o, o + 6), ("ed", 0, 6), ("ed", 8, 14), Op.mult)
+        ts(("nk", 0, 12), ("ed2", 0, 12), -8192.0, Op.mult, 8192.0, Op.add)
+        tt(("key", 0, 12), ("cl", 0, 12), ("nk", 0, 12), Op.add)
+        ts(("key1", 0, 12), ("key", 0, 12), 1.0, Op.add)
+        ts(("kh", 0, 12), ("key", 0, 12), 6, Op.arith_shift_right)
+        ts(("kh", 12, 24), ("key", 0, 12), 63, Op.bitwise_and)
+        ts(("khb", 0, 12), ("kh", 0, 12), 0.25, Op.mult)
+        ts(("khb", 16, 28), ("kh", 12, 24), 1.0 / 256, Op.mult)
+        ts(("sb", 0, 6), ("si", 0, 6), -2.0, Op.add)
+        cp(("sb", 8, 14), ("si", 8, 14))
+        seq = []
+        for j in range(16):
+            o = ("h0", j, 192, 16)
+            seq += [(o, LJ("LB", j), ("khb", 0, 12), True, False), (o, LJ("LB", j), ("khb", 16, 28), False, True)]
+        mm(seq, [full("LB"), ("khb", 0, 12), ("khb", 16, 28)], [("h0", 0, 192)])
+        mm([(("k0", j, 96, 16), LJ("LB", j), ("sb", 8, 14), True, True) for j in range(16)],
+           [full("LB"), ("sb", 8, 14)], [("k0", 0, 96)])
+        mm([(("k1", j, 96, 16), LJ("LB", j), ("sb", 0, 6), True, True) for j in range(16)],
+           [full("LB"), ("sb", 0, 6)], [("k1", 0, 96)])
+        mm([(("h1", 0, 96), M("CA"), ("dd", 0, 96), True, False), (("h1", 0, 96), M("CA"), (src, 0, 96), False, True)],
+           [M("CA"), ("dd", 0, 96), (src, 0, 96)], [("h1", 0, 96)])
+        for x in range(12):
+            J = x % 6
+            act(("LK", 96 * x, 96 * x + 96), ("LM", 96 * J, 96 * J + 96), Fn.Copy, bias=-1.0, scale=("key1", x, x + 1))
+        act(("mf", 0, 96), ("k1", 0, 96), Fn.Copy)
+        ts(("mk1", 0, 96), ("k0", 0, 96), KK, Op.is_equal)
+        tt(("cm", 0, 96), ("h1", 0, 96), ("mk1", 0, 96), Op.mult)
+        mm([(("k0", 0, 96), M("ISY"), (src, 0, 96), True, False), (("k0", 0, 96), M("RS"), ("cm", 0, 96), False, True)],
+           [M("ISY"), M("RS"), (src, 0, 96), ("cm", 0, 96)], [("k0", 0, 96)])
+        for x in range(12):
+            w = x // 6
+            e = ("EQ", 96 * x, 96 * x + 96)
+            tt(e, ("LK", 96 * x, 96 * x + 96), ("h0", 96 * w, 96 * w + 96), Op.is_equal)
+            act(e, e, Fn.Copy, accum=("CNT", x, x + 1))
+        cp(("Eb", 0, 96), ("k0", 0, 96))
+        ts(("w1", 12, 24), ("CNT", 0, 12), 0.0, Op.is_equal)
+        tt(("w1", 24, 36), ("cl", 0, 12), ("DU", 0, 12), Op.subtract)
+        tt(("w1", 36, 48), ("w1", 12, 24), ("ed2", 0, 12), Op.mult)
+        tt(("w1", 48, 60), ("w1", 24, 36), ("w1", 36, 48), Op.mult)
+        tt(("w1", 12, 24), ("w1", 48, 60), ("DU", 0, 12), Op.add)
+        cp(("OE", 0, 12), ("w1", 12, 24))
+        oF, oB, full_w = ("OE", 0, 6), ("OE", 6, 12), ("mkT", 0, MKW)
+        emit("v", lambda: g.vector.tensor_copy(win(oF, MKW), ap(("Eb", 0, 96))), [oF, ("Eb", 0, 96)], [full_w])
+        emit("v", lambda: g.vector.tensor_copy(ap(("vb", 0, 96)), win(oB, MKW)), [oB, full_w], [("vb", 0, 96)])
+        mm([(("h1", 0, 96), M("ISY"), ("vb", 0, 96), True, False), (("h1", 0, 96), M("DN"), ("vb", 0, 96), False, False),
+            (("h1", 0, 96), M("R12"), ("mf", 0, 96), False, True)],
+           [M("ISY"), M("DN"), M("R12"), ("vb", 0, 96), ("mf", 0, 96)], [("h1", 0, 96)])
+        cp(("Sb", 0, 96), ("h1", 0, 96))
+        emit("v", lambda: g.vector.tensor_copy(win(oB, MKW), ap(("Sb", 0, 96))), [oB, ("Sb", 0, 96)], [full_w])
+
+    search("qN", True)
+    close("qN", lambda x, y: "qB" if x // NB == rank else "qA", send)
+    consts_edits()
+    edits("qN")
+    arrivals()
+    search("qB", False)
+
+    def out(c):
+        b = chunk("qF", c)
+        emit("s", lambda: g.sync.dma_start(T.yq[:, c * CH:c * CH + CH], ap(b)), [b], [], "dy%d" % c)
+
+    close("qB", lambda x, y: "qF", out)
+    ts(("y1", 0, 96), ("B", 0, 96), 0.0, Op.is_gt)
+    ts(("y2", 0, 96), ("Hb", 0, 96), 1.0, Op.add)
+    tt(("y3", 0, 96), ("y1", 0, 96), ("y2", 0, 96), Op.mult)
+    ts(("yS", 0, 96), ("y3", 0, 96), -1.0, Op.add)
+    emit("s", lambda: g.sync.dma_start(T.yb[:], ap(("yS", 0, 96))), [("yS", 0, 96)], [], "dyb")
+    await_all("g", list(total.items()) + [("sent", nsent[0])])

@@ -4,6 +4,7 @@ W, K, NB = 4096, 1536, 384
 CH, NJ = 768, 48
 MKW = W + 128
 LN256 = 5.545177444479562
+CYC, PEC, WAKE, SLACK = 0.00083, 0.00042, 0.17, 0.04
 
 _sets = ["LX", "LY", "LN", "LV0", "LV1", "LV2", "LV3", "LB", "BIG"]
 _mats = ["JR", "JA", "JP", "BD", "ID", "HI", "NI", "R0", "ISY", "SRC", "CAQ", "CA", "RS", "DN", "R12"]
@@ -24,7 +25,7 @@ def _add(dtype, **widths):
 
 
 _add("bfloat16", wS=2, Aw=384, tm=288, Lb=96, khb=32, sb=16, cm=96, Eb=96, vb=96, mf=96, Sb=96)
-_add("int32", pi=1, ki=1, ci=4, U=192, UA=192, P=96, Kk=96, Wd=96, S=96, H=96, codeS=384, ch=96, B=96, Hb=96, Li=96,
+_add("int32", pi=1, ki=1, ci=4, U=288, UA=288, P=96, Wd=96, S=96, H=96, codeS=384, ch=96, B=96, Hb=96, Li=96, y0=96,
      fc=192, f1=32, FB=12, cl=12, key=12, kh=24, si=16)
 _add("float32", col=32, E256=16, geo=64, IT=96, LM=576, DU=12, hitS=384, th=96, m97=96, mt=192, y1=96, y2=96, y3=96, yS=96,
      al=192, ms=192, ed=32, ed2=12, nk=12, key1=12, LK=1152, EQ=1152, CNT=12, w1=64, mk1=96)
@@ -32,8 +33,8 @@ _add("uint16", OFF=96, OB=96, OE=12)
 BANKS = ("g00", "g01", "g10", "g11", "h0", "h1", "k0", "k1")
 for _n in BANKS:
     SCRATCH[_n] = ("psum", [128, 512], "float32")
-SEMAPHORES = ["sV", "sA", "sP", "sG", "dw", "dq0", "dq1", "dm0", "dm1", "dy0", "dy1", "dyb",
-              "arr0", "arr1", "arr2", "arr3", "sent", "rin", "rls"]
+SEMAPHORES = ["sV", "sA", "sP", "sG", "dw", "dq0", "dq1", "dq2", "dq3", "dm0", "dm1", "dy0", "dy1", "dy2", "dy3",
+              "db0", "db1", "db2", "db3", "arr0", "arr1", "arr2", "arr3", "sent", "rin", "rls"]
 
 
 def relay_of(src, dst, cores, topo):
@@ -50,6 +51,10 @@ def relay_of(src, dst, cores, topo):
             return near[0] if k % 2 == 0 else far[0]
         k += 1
     return None
+
+
+def held_order(rank):
+    return [(rank + k) % 4 for k in (0, 1, 3, 2)], [(rank - k) % 4 for k in (0, 1, 3, 2)]
 
 
 def count(mask):
@@ -75,94 +80,130 @@ def rank_program(g, core, T, topo):
                 m_in = off_chip_mask(a, cores, topo) & topo.mask(a, core)
                 m_out = topo.mask(core, b)
                 rid, pid = topo.addr(b, core)
+                p = NB * held_order(T.rank_of(b))[1].index(r)
                 g.wait_ge(T.sem.rin, count(m_in))
-                g.remote_dma(T.qB[:, NB * r:NB * r + NB], T.land[:], T.sem["arr%d" % r], T.sem.rls, pid, rid, m_out)
+                g.remote_dma(T.qB[:, p:p + NB], T.land[:], T.sem["arr%d" % r], T.sem.rls, pid, rid, m_out)
                 g.wait_ge(T.sem.rls, count(m_out))
         return
 
     Q = {"v": g.vector, "a": g.scalar, "p": g.tensor, "g": g, "s": g.sync}
     SEM = {"v": "sV", "a": "sA", "p": "sP", "g": "sG"}
-    cnt = {"v": 0, "a": 0, "p": 0, "g": 0}
-    clock = {q: {} for q in Q}
-    clkat = {}
+    ops = []
     rec = {}
-    bank = {}
-    total = {}
 
-    def see(q, ev):
-        c = clock[q]
-        for s, x in clkat.get(ev, {}).items():
-            if c.get(s, 0) < x:
-                c[s] = x
-        if c.get(ev[0], 0) < ev[1]:
-            c[ev[0]] = ev[1]
-
-    def await_all(q, evs):
-        best = {}
-        for s, x in evs:
-            best[s] = max(best.get(s, 0), x)
-        todo = [(s, x) for s, x in best.items() if clock[q].get(s, 0) < x]
-        keep = []
-        for e in todo:
-            if not any(o != e and clkat.get(o, {}).get(e[0], 0) >= e[1] for o in todo):
-                keep.append(e)
-        for s, x in keep:
-            Q[q].wait_ge(T.sem[s], x)
-            see(q, (s, x))
-
-    def conflicts(q, reads, writes, dma):
-        evs = []
+    def emit(q, fn, reads, writes, sem=None, cost=0.1, ev=None, after=()):
+        i = len(ops)
+        waits, order = set(after), set()
         for kind, lst in (("r", reads), ("w", writes)):
             for b in lst:
                 nm, lo, hi = b[0], b[1], b[2]
+                r = rec.setdefault(nm, [])
                 if nm in BANKS:
-                    for q2, st in bank.get(nm, {}).items():
-                        if q2 != q:
-                            evs.append(st[0])
-                        elif q != "p" and st[1] is not None:
-                            evs.append(st[1])
-                    continue
-                for l2, h2, q2, ev, k2 in rec.get(nm, ()):
-                    if l2 < hi and lo < h2 and (kind == "w" or k2 == "w"):
-                        if k2 == "r" and q2 == q and not dma:
+                    for x in r:
+                        if x[3] == i:
                             continue
-                        evs.append(ev)
-        return evs
+                        if x[2] != q or (x[4] == "w" and q != "p"):
+                            waits.add(x[3])
+                        else:
+                            order.add(x[3])
+                    r[:] = [x for x in r if x[2] == q or x[3] == i]
+                else:
+                    for x in r:
+                        if x[3] != i and x[0] < hi and lo < x[1] and (kind == "w" or x[4] == "w"):
+                            waits.add(x[3])
+                    if kind == "w":
+                        r[:] = [x for x in r if not (lo <= x[0] and x[1] <= hi)]
+                r.append((lo, hi, q, i, kind))
+        ops.append((q, fn, sem, cost, waits, order - waits, ev))
+        return i
 
-    def note(q, reads, writes, ev, dma):
-        qn = "dma" if dma else q
-        for b in reads:
-            if b[0] in BANKS:
-                st = bank.setdefault(b[0], {}).get(q, (None, None))
-                bank[b[0]][q] = (ev, st[1])
-            else:
-                lst = rec.setdefault(b[0], [])
-                lst[:] = [x for x in lst if not (x[4] == "r" and x[2] == qn and not dma and b[1] <= x[0] and x[1] <= b[2])]
-                lst.append((b[1], b[2], qn, ev, "r"))
-        for b in writes:
-            if b[0] in BANKS:
-                bank.setdefault(b[0], {})[q] = (ev, ev)
-            else:
-                lst = rec.setdefault(b[0], [])
-                lst[:] = [x for x in lst if not (b[1] <= x[0] and x[1] <= b[2])]
-                lst.append((b[1], b[2], qn, ev, "w"))
+    def place():
+        n = len(ops)
+        succ = [[] for _ in ops]
+        need = [0] * n
+        for i in range(n):
+            for d in ops[i][4] | ops[i][5]:
+                succ[d].append(i)
+                need[i] += 1
+        prio = [0.0] * n
+        for i in reversed(range(n)):
+            prio[i] = ops[i][3] + max([prio[j] + (WAKE if i in ops[j][4] else 0.0) for j in succ[i]] + [0.0])
+        at = [0.0] * n
+        ready = [i for i in range(n) if need[i] == 0]
+        free = {}
+        seq = []
+        while ready:
+            st = [max(free.get(ops[i][0], 0.0), at[i]) for i in ready]
+            t = min(st)
+            q = ops[ready[st.index(t)]][0]
+            i = -max((prio[i], -i) for i, x in zip(ready, st) if ops[i][0] == q and x <= t + SLACK)[1]
+            t = max(free.get(q, 0.0), at[i])
+            ready.remove(i)
+            seq.append(i)
+            end = t + ops[i][3]
+            free[q] = t + 0.05 if ops[i][2] is not None else end
+            for j in succ[i]:
+                at[j] = max(at[j], end + WAKE if i in ops[j][4] else t)
+                need[j] -= 1
+                if need[j] == 0:
+                    ready.append(j)
+        return seq
 
-    def emit(q, fn, reads, writes, sem=None):
-        await_all(q, conflicts(q, reads, writes, sem is not None))
-        ins = fn()
-        if sem is None:
-            cnt[q] += 1
-            ev = (SEM[q], cnt[q])
-            ins.then_inc(T.sem[SEM[q]], 1)
-        else:
-            ev = (sem, 16)
-            ins.then_inc(T.sem[sem], 16)
-        total[ev[0]] = ev[1]
-        c = dict(clock[q])
-        c[ev[0]] = ev[1]
-        clkat[ev] = c
-        note(q, reads, writes, ev, sem is not None)
-        return ev
+    def issue(seq):
+        cnt = {"v": 0, "a": 0, "p": 0, "g": 0}
+        clock = {q: {} for q in Q}
+        clkat, evs, total = {}, {}, {}
+
+        def see(q, ev):
+            c = clock[q]
+            for s, x in list(clkat.get(ev, {}).items()) + [ev]:
+                if c.get(s, 0) < x:
+                    c[s] = x
+
+        def await_all(q, want):
+            best = {}
+            for s, x in want:
+                best[s] = max(best.get(s, 0), x)
+            todo = [(s, x) for s, x in best.items() if clock[q].get(s, 0) < x]
+            for e in [e for e in todo if not any(o != e and clkat.get(o, {}).get(e[0], 0) >= e[1] for o in todo)]:
+                Q[q].wait_ge(T.sem[e[0]], e[1])
+                see(q, e)
+
+        for i in seq:
+            q, fn, sem, cost, waits, order, ev = ops[i]
+            if fn is None:
+                evs[i] = ev
+                clkat[ev] = {}
+                total[ev[0]] = ev[1]
+                continue
+            await_all(q, [evs[d] for d in waits if evs.get(d) is not None])
+            ins = fn()
+            if ev is not None:
+                total[ev[0]] = total.get(ev[0], 0) + ev[1]
+                continue
+            if sem is None:
+                cnt[q] += 1
+                evs[i] = (SEM[q], cnt[q])
+                ins.then_inc(T.sem[SEM[q]], 1)
+            else:
+                evs[i] = (sem, 16)
+                ins.then_inc(T.sem[sem], 16)
+            total[evs[i][0]] = evs[i][1]
+            c = dict(clock[q])
+            c[evs[i][0]] = evs[i][1]
+            clkat[evs[i]] = c
+        await_all("g", list(total.items()))
+
+    def wide(b):
+        return (b[2] - b[1] + (b[3] - 1 if len(b) > 3 else 0)) // (b[3] if len(b) > 3 else 1)
+
+    def cost(out, ins, two=False):
+        n = wide(out)
+        if two:
+            n *= 1 if any(b[0] in BANKS for b in ins) else 2
+        elif all(SCRATCH[b[0]][2] in ("bfloat16", "uint16") for b in [out] + ins):
+            n /= 2
+        return max(64, n) * CYC + 0.03
 
     def ap(b):
         if len(b) > 3:
@@ -173,18 +214,18 @@ def rank_program(g, core, T, topo):
         return isinstance(x, tuple)
 
     def tt(out, a, b, op):
-        return emit("v", lambda: g.vector.tensor_tensor(ap(out), ap(a), ap(b), op), [a, b], [out])
+        return emit("v", lambda: g.vector.tensor_tensor(ap(out), ap(a), ap(b), op), [a, b], [out], cost=cost(out, [a, b], True))
 
     def ts(out, a, s1, op0, s2=None, op1=None):
         rd = [a] + [s for s in (s1, s2) if isap(s)]
         x1 = ap(s1) if isap(s1) else s1
         x2 = ap(s2) if isap(s2) else s2
         if op1 is None:
-            return emit("v", lambda: g.vector.tensor_scalar(ap(out), ap(a), x1, None, op0), rd, [out])
-        return emit("v", lambda: g.vector.tensor_scalar(ap(out), ap(a), x1, x2, op0, op1), rd, [out])
+            return emit("v", lambda: g.vector.tensor_scalar(ap(out), ap(a), x1, None, op0), rd, [out], cost=cost(out, [a]))
+        return emit("v", lambda: g.vector.tensor_scalar(ap(out), ap(a), x1, x2, op0, op1), rd, [out], cost=cost(out, [a]))
 
     def cp(out, a):
-        return emit("v", lambda: g.vector.tensor_copy(ap(out), ap(a)), [a], [out])
+        return emit("v", lambda: g.vector.tensor_copy(ap(out), ap(a)), [a], [out], cost=cost(out, [a]))
 
     def fill(out, x):
         return emit("v", lambda: g.vector.memset(ap(out), x), [], [out])
@@ -200,7 +241,7 @@ def rank_program(g, core, T, topo):
         if accum is not None:
             kw["accum_out"] = ap(accum)
             wr = [out, accum]
-        return emit("a", lambda: g.scalar.activation(ap(out), ap(a), fn, **kw), rd, wr)
+        return emit("a", lambda: g.scalar.activation(ap(out), ap(a), fn, **kw), rd, wr, cost=wide(out) * CYC + 0.05)
 
     def mm(seq, reads, writes):
         def go():
@@ -208,13 +249,16 @@ def rank_program(g, core, T, topo):
             for o, l, r, st, sp in seq:
                 ins = g.tensor.matmul(ap(o), ap(l), ap(r), st, sp)
             return ins
-        return emit("p", go, reads, writes)
+        return emit("p", go, reads, writes, cost=sum(max(64, wide(o)) for o, l, r, st, sp in seq) * PEC + 0.03)
 
     def LJ(nm, j):
         return (nm, 128 * j, 128 * j + 128)
 
     def M(nm):
         return (nm, 0, 128)
+
+    def full(nm):
+        return (nm, 0, 2048)
 
     def word(nm, out, src, base, w, extra=None, strided=True):
         seq = []
@@ -223,17 +267,18 @@ def rank_program(g, core, T, topo):
         for j in range(16):
             r = (src, base + j, base + 16 * w, 16) if strided else (src, base + w * j, base + w * (j + 1))
             seq.append((out, LJ(nm, j), r, extra is None and j == 0, j == 15))
-        rd = [(nm, 0, 2048), (src, base, base + 16 * w)]
+        rd = [full(nm), (src, base, base + 16 * w)]
         if extra is not None:
             rd += [extra[0], extra[1]]
         return mm(seq, rd, [out])
 
-    emit("a", lambda: g.scalar.dma_start(ap(("wS", 0, 2)), T.wt[:]), [], [("wS", 0, 2)], "dw")
-    for c in range(2):
-        emit("s", lambda: g.sync.dma_start(ap(("qN", CH * c, CH * c + CH)), T.qs[:, CH * c:CH * c + CH]), [],
-             [("qN", CH * c, CH * c + CH)], "dq%d" % c)
-    emit("a", lambda: g.scalar.dma_start(ap(("mkT", 0, 2048)), T.mk[:, 0:2048]), [], [("mkT", 0, 2048)], "dm0")
-    emit("s", lambda: g.sync.dma_start(ap(("mkT", 2048, W)), T.mk[:, 2048:W]), [], [("mkT", 2048, W)], "dm1")
+    goes, came = held_order(rank)
+    emit("a", lambda: g.scalar.dma_start(ap(("wS", 0, 2)), T.wt[:]), [], [("wS", 0, 2)], "dw", 2.0)
+    for p in range(4):
+        b = ("qN", NB * p, NB * p + NB)
+        emit("s", lambda b=b, x=NB * goes[p]: g.sync.dma_start(ap(b), T.qs[:, x:x + NB]), [], [b], "dq%d" % p, 2.5 + 0.5 * p)
+    emit("a", lambda: g.scalar.dma_start(ap(("mkT", 0, 2048)), T.mk[:, 0:2048]), [], [("mkT", 0, 2048)], "dm0", 7.0)
+    emit("s", lambda: g.sync.dma_start(ap(("mkT", 2048, W)), T.mk[:, 2048:W]), [], [("mkT", 2048, W)], "dm1", 7.0)
 
     def C(i):
         return ("col", i, i + 1)
@@ -241,6 +286,7 @@ def rank_program(g, core, T, topo):
     RC = [C(12 + r) for r in range(4)]
     KJ = [C(16 + J) for J in range(6)]
     KLT = C(22)
+    T2, T3, T4, T5 = [C(24 + i) for i in range(4)]
 
     def iota(out, pattern, base, cm, flag=True):
         if flag:
@@ -248,7 +294,8 @@ def rank_program(g, core, T, topo):
         return emit("g", lambda: g.iota(ap(out), pattern, base, cm), [], [out])
 
     def pick(out, a, pattern, op, x, base, cm):
-        return emit("g", lambda: g.affine_select(ap(out), ap(a), pattern, op, x, base, cm), [a], [out])
+        return emit("g", lambda: g.affine_select(ap(out), ap(a), pattern, op, x, base, cm), [a], [out],
+                    cost=0.17 + 2 * wide(out) * CYC)
 
     iota(("pi", 0, 1), [[0, 1]], 0, 1, False)
     iota(M("JR"), [[0, 8], [1, 16]], 0, 0)
@@ -265,13 +312,11 @@ def rank_program(g, core, T, topo):
     ts(M("R0"), M("BD"), RC[0], Op.mult, 256.0, Op.mult)
     for j in range(16):
         ts(LJ("BIG", j), M("JP"), float(j), Op.is_equal)
-
-    def full(nm):
-        return (nm, 0, 2048)
     ts(full("LX"), full("BIG"), ("wS", 0, 1), Op.mult)
     ts(full("LY"), full("BIG"), ("wS", 1, 2), Op.mult)
     act(full("LV0"), full("BIG"), Fn.Copy, scale=RC[0])
-    pick(full("LV1"), full("BIG"), [[0, 16], [-16, 8], [0, 16]], Op.is_equal, 0.0, -13, 1)
+    for r in (1, 2):
+        pick(full("LV%d" % r), full("BIG"), [[0, 16], [-16, 8], [0, 16]], Op.is_equal, 0.0, -12 - r, 1)
     iota(M("SRC"), [[0, 8], [1, 4], [1, 4]], 13, 0)
     iota(("IT", 0, 96), [[1, 96]], 0, 0)
     iota(("w1", 0, 12), [[0, 2], [16, 6]], W, 0)
@@ -285,15 +330,10 @@ def rank_program(g, core, T, topo):
         tt(("geo", 48, 60), ("geo", 32, 44), ("E256", 0, 12), Op.mult)
         emit("v", lambda: g.vector.tensor_reduce(ap(WN), ap(("geo", 48, 60)), AxisListType.X, Op.add), [("geo", 48, 60)], [WN])
         ts(full("LN"), full("BIG"), WN, Op.mult, 1.0 / 256, Op.mult)
-        ts(full("LV2"), full("BIG"), RC[2], Op.mult)
         ts(full("LV3"), full("BIG"), RC[3], Op.mult)
         ts(M("NI"), M("ID"), -1.0, Op.mult)
-
-    def consts_bcast():
         for j in range(16):
             ts(LJ("LB", j), M("BD"), ("E256", j, j + 1), Op.mult)
-
-    def consts_late():
         ts(M("HI"), M("ID"), 0.5, Op.mult)
         ts(T0, KC, 11.5, Op.is_gt, -100000.0, Op.mult)
         ts(T1, NBI, 128.0, Op.subtract)
@@ -306,15 +346,15 @@ def rank_program(g, core, T, topo):
         ts(M("CAQ"), M("SRC"), KC, Op.is_equal)
         tt(M("CA"), M("CAQ"), M("BD"), Op.mult)
         ts(("ci", 0, 1), ("ki", 0, 1), 3, Op.bitwise_and)
-        ts(T0, KC, 11.5, Op.is_gt, 50.0, Op.mult)
-        ts(T1, ("ci", 0, 1), 12.0, Op.add)
-        tt(RCOL, T0, T1, Op.add)
+        ts(T2, KC, 11.5, Op.is_gt, 50.0, Op.mult)
+        ts(T3, ("ci", 0, 1), 12.0, Op.add)
+        tt(RCOL, T2, T3, Op.add)
         ts(M("RS"), M("JP"), RCOL, Op.is_equal)
         ts(("ci", 1, 2), ("ki", 0, 1), 2, Op.arith_shift_right)
         ts(KK, ("ci", 1, 2), -256.0, Op.mult, 768.0, Op.add)
-        ts(T0, KC, 11.5, Op.is_lt, 50.0, Op.mult)
-        ts(T1, KC, 1.0, Op.add)
-        tt(KP1, T0, T1, Op.add)
+        ts(T4, KC, 11.5, Op.is_lt, 50.0, Op.mult)
+        ts(T5, KC, 1.0, Op.add)
+        tt(KP1, T4, T5, Op.add)
         ts(M("DN"), M("JP"), KP1, Op.is_equal)
         ts(R120, RC[0], 1.0 / 256, Op.mult)
         ts(M("R12"), M("ID"), R120, Op.mult)
@@ -328,8 +368,8 @@ def rank_program(g, core, T, topo):
         return (nm, lo, lo + NJ)
 
     def half(nm, c, h):
-        lo = c * CH + h * 384
-        return (nm, lo, lo + 384)
+        lo = c * CH + h * NB
+        return (nm, lo, lo + NB)
 
     def chunk(nm, c):
         return (nm, c * CH, c * CH + CH)
@@ -342,8 +382,8 @@ def rank_program(g, core, T, topo):
             seq = []
             for x in range(8):
                 seq.append(((bk, x * NJ, x * NJ + NJ), M("ID"), (src, c * CH + 8 * h + x, c * CH + CH, 16), True, True))
-            mm(seq, [M("ID"), chunk(src, c)], [(bk, 0, 384)])
-            act(half("qj", c, h), (bk, 0, 384), Fn.Identity, bias=PB)
+            mm(seq, [M("ID"), chunk(src, c)], [(bk, 0, NB)])
+            act(half("qj", c, h), (bk, 0, NB), Fn.Identity, bias=PB)
 
     def lengths(c, src, rs):
         for r in rs:
@@ -362,11 +402,11 @@ def rank_program(g, core, T, topo):
                     seq.append((o, M("R0"), (src, c * CH + j, c * CH + CH, 16), True, True))
                 else:
                     seq.append((o, LJ("LB", j), m, True, True))
-            mm(seq, [M("R0"), chunk(src, c)] if s == 1 else [full("LB"), m], [(gb(c, h), 0, 384)])
+            mm(seq, [M("R0"), chunk(src, c)] if s == 1 else [full("LB"), m], [(gb(c, h), 0, NB)])
 
     def V1(c):
         for h in range(2):
-            tt(half("zp", c, h), half("qj", c, h), (gb(c, h), 0, 384), Op.min)
+            tt(half("zp", c, h), half("qj", c, h), (gb(c, h), 0, NB), Op.min)
 
     def A1(c):
         for h in range(2):
@@ -383,31 +423,27 @@ def rank_program(g, core, T, topo):
         word("LY", ("h%d" % c, NJ, 2 * NJ), "zz", c * CH, NJ, strided=False)
 
     def V2(c):
-        hb = "h%d" % c
-        u = ("U", c * 96, c * 96 + 96)
-        ua = ("UA", c * 96, c * 96 + 96)
-        return [lambda: cp(u, (hb, 0, 96)),
-                lambda: tt(sm("Wd", c), (hb, NJ, 96), sm("m97", c), Op.add),
-                lambda: ts(ua, u, 4095, Op.bitwise_and),
-                lambda: tt(sm("P", c), ("UA", c * 96, c * 96 + NJ), ("UA", c * 96 + NJ, c * 96 + 96), Op.mult),
-                lambda: ts(sm("Kk", c), sm("P", c), 5, Op.arith_shift_right),
-                lambda: tt(sm("S", c), sm("Kk", c), sm("Wd", c), Op.add),
-                lambda: ts(sm("H", c), sm("S", c), 4095, Op.bitwise_and),
-                lambda: cp(sm("OFF", c), sm("H", c))]
+        hb, o = "h%d" % c, c * 3 * NJ
+        cp(("U", o, o + 2 * NJ), (hb, 0, 2 * NJ))
+        tt(sm("U", c, 2, 3), (hb, NJ, 2 * NJ), sm("m97", c), Op.add)
+        ts(("UA", o, o + 3 * NJ), ("U", o, o + 3 * NJ), 4095, Op.bitwise_and)
+        tt(sm("P", c), sm("UA", c, 0, 3), sm("UA", c, 1, 3), Op.mult)
+        ts(sm("Wd", c), sm("UA", c, 2, 3), 32.0, Op.mult, -131072.0, Op.add)
+        tt(sm("S", c), sm("P", c), sm("Wd", c), Op.add)
+        ts(sm("H", c), sm("S", c), 5, Op.arith_shift_right, 4095, Op.bitwise_and)
+        cp(sm("OFF", c), sm("H", c))
 
     def win(off, w=W):
         return T.mkT[:, 0:w].indirect(ap(off))
 
-    def V3(c, src):
-        o, off, q = chunk("nn", c), sm("OFF", c), chunk(src, c)
-        emit("v", lambda: g.vector.tensor_tensor(ap(o), win(off), ap(q), Op.not_equal), [("mkT", 0, W), off, q], [o])
+    def gathered(o, off, q, op):
+        emit("v", lambda: g.vector.tensor_tensor(ap(o), win(off), ap(q), op), [("mkT", 0, W), off, q], [o],
+             cost=0.08 + 1.5 * CYC * wide(o))
 
     def A3(c):
         o, off = chunk("vv", c), sm("OFF", c)
-        emit("a", lambda: g.scalar.activation(ap(o), win(off), Fn.Copy), [("mkT", 0, W), off], [o])
-
-    def P3(c):
-        word("LN", ("k%d" % c, 0, NJ), "nn", c * CH, NJ)
+        emit("a", lambda: g.scalar.activation(ap(o), win(off), Fn.Copy), [("mkT", 0, W), off], [o],
+             cost=0.1 + 1.5 * CYC * wide(o))
 
     def held(c, w):
         return ("k%d" % c, NJ, 2 * NJ) if w == 0 else ("h%d" % c, (w - 1) * NJ, w * NJ)
@@ -416,156 +452,105 @@ def rank_program(g, core, T, topo):
         for w in range(4 - s):
             word("LV%d" % w, held(c, w), "vv", c * CH, NJ, extra=(M("NI"), sm("Aw", c, s + w, 4)))
 
-    def tail(c, s):
+    def V4(c, s):
         hit, code = sm("hitS", c, s - 1, 4), sm("codeS", c, s - 1, 4)
-        first = [lambda: tt(hit, ("k%d" % c, 0, NJ), sm("th", c), Op.is_gt),
-                 lambda: tt(code, sm("H", c), sm("mt", c, s % 2, 2), Op.add)]
-        mul, add = [], []
+        tt(code, sm("H", c), sm("mt", c, s % 2, 2), Op.add)
+        tt(hit, ("k%d" % c, 0, NJ), sm("th", c), Op.is_gt)
         for w in range(4 - s):
             t = ("tm", c * 144 + w * NJ, c * 144 + w * NJ + NJ)
-            a = sm("Aw", c, s + w, 4)
-            mul.append(lambda o=held(c, w), t=t: tt(t, o, hit, Op.mult))
-            add.append(lambda a=a, t=t: tt(a, a, t, Op.add))
-        if s == 1:
-            mb = [lambda: tt(sm("B", c), code, hit, Op.mult)]
-        else:
-            mb = [lambda: tt(sm("ch", c), code, hit, Op.mult), lambda: tt(sm("B", c), sm("B", c), sm("ch", c), Op.max)]
-        if s < 4:
-            return first + mul[:1], mb[:1] + add[:1] + mul[1:] + add[1:], mb[1:]
-        return first, mb, []
-
-    def run(*lists):
-        for x in range(max(len(l) for l in lists)):
-            for l in lists:
-                if x < len(l):
-                    l[x]()
+            tt(t, held(c, w), hit, Op.mult)
+            tt(sm("Aw", c, s + w, 4), sm("Aw", c, s + w, 4), t, Op.add)
+        tt(sm("B" if s == 1 else "ch", c), code, hit, Op.mult)
+        if s > 1:
+            tt(sm("B", c), sm("B", c), sm("ch", c), Op.max)
 
     def La(c, src):
         ts(sm("Li", c), sm("B", c), 12, Op.arith_shift_right, 15, Op.bitwise_and)
         ts(sm("Hb", c), sm("B", c), 4095, Op.bitwise_and)
         cp(sm("Lb", c), sm("Li", c))
         cp(sm("OB", c), sm("Hb", c))
-        for h, lo, n in ((0, 0, 32), (1, 32, 16)):
-            r = ("Lb", c * NJ + lo, c * NJ + lo + n)
-            bk = (gb(c, h), 0, 16 * n)
-            mm([((gb(c, h), j, 16 * n, 16), LJ("LB", j), r, True, True) for j in range(16)], [full("LB"), r], [bk])
+        for h in range(2):
+            r = ("Lb", c * NJ + 24 * h, c * NJ + 24 * h + 24)
+            bk = (gb(c, h), 0, NB)
+            mm([((gb(c, h), j, NB, 16), LJ("LB", j), r, True, True) for j in range(16)], [full("LB"), r], [bk])
             act(bk, bk, Fn.Sign, bias=LBI)
-        o, off, q = chunk("dd", c), sm("OB", c), chunk(src, c)
-        emit("v", lambda: g.vector.tensor_tensor(ap(o), win(off), ap(q), Op.subtract), [("mkT", 0, W), off, q], [o])
+            gathered(half("dd", c, h), ("OB", c * NJ + 24 * h, c * NJ + 24 * h + 24), half(src, c, h), Op.subtract)
 
-    def Lb(c, src, dest):
-        for h, lo, hi in ((0, c * CH, c * CH + 512), (1, c * CH + 512, c * CH + CH)):
-            bk = (gb(c, h), 0, hi - lo)
-            tt(("sd", lo, hi), ("dd", lo, hi), bk, Op.mult)
-            mm([(bk, M("ID"), (src, lo, hi), True, False), (bk, M("HI"), ("dd", lo, hi), False, False),
-                (bk, M("HI"), ("sd", lo, hi), False, True)],
-               [M("ID"), M("HI"), (src, lo, hi), ("dd", lo, hi), ("sd", lo, hi)], [bk])
-            cuts = [lo] + [x for x in range(0, K, NB) if lo < x < hi] + [hi]
-            for x, y in zip(cuts[:-1], cuts[1:]):
-                act((dest(x, y), x, y), (gb(c, h), x - lo, y - lo), Fn.Copy)
+    def Lb(c, h, src, to):
+        bk, d, sd, q = (gb(c, h), 0, NB), half("dd", c, h), half("sd", c, h), half(src, c, h)
+        tt(sd, d, bk, Op.mult)
+        mm([(bk, M("ID"), q, True, False), (bk, M("HI"), d, False, False), (bk, M("HI"), sd, False, True)],
+           [M("ID"), M("HI"), q, d, sd], [bk])
+        act(half(to, c, h), bk, Fn.Copy)
 
-    def search(src, first):
-        for c in range(2):
-            jmajor(c, src)
-            P1(c, 1, src)
-            V1(c)
-            A1(c)
-        if first:
-            consts_search()
-        for c in range(2):
-            lengths(c, src, [0])
-            A2(c, 1)
-            P2(c)
-        late0 = late1 = []
+    def search(src):
         for s in range(1, 5):
-            if s > 1:
-                V1(0)
-                A1(0)
-                f1, n1, late1 = tail(1, s - 1)
-                run(f1, late0)
-                run(n1)
-                P1(1, s, src)
-                A2(1, s)
-                P2(0)
-                V1(1)
-                A1(1)
-                P2(1)
-            else:
-                for c in range(2):
+            for c in range(2):
+                if s == 1:
+                    jmajor(c, src)
+                P1(c, s, src)
+                if s == 1:
+                    lengths(c, src, [0])
+                A2(c, s)
+                V1(c)
+                A1(c)
+                P2(c)
+                if s == 1:
                     lengths(c, src, [1, 2, 3])
-            run(V2(0), late1)
-            V3(0, src)
-            if s < 4:
-                A3(0)
-            P3(0)
-            P4(0, s)
-            run(V2(1))
-            if first and s == 1:
-                consts_bcast()
-                consts_late()
-            f0, n0, late0 = tail(0, s)
-            run(f0)
-            run(n0[:2])
-            if s < 4:
-                P1(0, s + 1, src)
-            V3(1, src)
-            if s < 4:
-                A3(1)
-                A2(0, s + 1)
-            P3(1)
-            P4(1, s)
-            late0 = n0[2:] + late0
-        run(late0)
+                V2(c)
+                gathered(chunk("nn", c), sm("OFF", c), chunk(src, c), Op.not_equal)
+                if s < 4:
+                    A3(c)
+                word("LN", ("k%d" % c, 0, NJ), "nn", c * CH, NJ)
+                P4(c, s)
+                V4(c, s)
 
     def close(src, dest, after):
-        La(0, src)
-        for part in tail(1, 4):
-            if part:
-                run(part)
-        Lb(0, src, dest)
-        after(0)
-        La(1, src)
-        Lb(1, src, dest)
-        after(1)
+        for c in range(2):
+            La(c, src)
+            for h in range(2):
+                Lb(c, h, src, dest(2 * c + h))
+                after(2 * c + h)
 
     omask = off_chip_mask(core, cores, topo)
-    nsent = [0]
+    sends = []
 
-    def send(c):
-        todo = [s for s in (2 * c, 2 * c + 1) if s != rank]
-        todo.sort(key=lambda s: relay_of(core, cores[s], cores, topo) is None)
-        for s in todo:
-            b = ("qA", NB * s, NB * s + NB)
-            await_all("g", conflicts("g", [b], [], True))
-            rel = relay_of(core, cores[s], cores, topo)
-            to = cores[s] if rel is None else rel
-            m = omask & topo.mask(core, to)
-            rid, pid = topo.addr(to, core)
-            if rel is None:
-                g.remote_dma(T.qB[:, NB * rank:NB * rank + NB], ap(b), T.sem["arr%d" % rank], T.sem.sent, pid, rid, m)
-            else:
-                g.remote_dma(T.land[:], ap(b), T.sem.rin, T.sem.sent, pid, rid, m)
-            nsent[0] += count(m)
+    def send(p):
+        s = goes[p]
+        if s == rank:
+            return
+        b = ("qA", NB * p, NB * p + NB)
+        rel = relay_of(core, cores[s], cores, topo)
+        to = cores[s] if rel is None else rel
+        m = omask & topo.mask(core, to)
+        rid, pid = topo.addr(to, core)
+        x = NB * held_order(s)[1].index(rank)
+        dst, sem = (T.land[:], "rin") if rel is not None else (T.qB[:, x:x + NB], "arr%d" % rank)
+        sends.append(emit("g", lambda: g.remote_dma(dst, ap(b), T.sem[sem], T.sem.sent, pid, rid, m), [b], [], None, 0.3,
+                          ("sent", count(m))))
 
     def arrivals():
-        for s in range(4):
+        for p in range(4):
+            s = came[p]
             if s != rank:
                 rel = relay_of(cores[s], core, cores, topo)
                 n = count(topo.mask(cores[s] if rel is None else rel, core))
-                ev = ("arr%d" % s, n)
-                clkat[ev] = {ev[0]: n}
-                total[ev[0]] = n
-                note("x", [], [("qB", NB * s, NB * s + NB)], ev, True)
+                emit("x%d" % s, None, [], [("qB", NB * p, NB * p + NB)], None, 4.0 if rel is None else 8.0, ("arr%d" % s, n),
+                     sends[:1] if p < 2 else sends)
 
     def edits(src):
-        ts(("al", 0, 192), ("Aw", 0, 192), 0.0, Op.is_gt)
-        tt(("ms", 0, 192), ("al", 0, 192), ("hitS", 0, 192), Op.subtract)
-        tt(("fc", 0, 192), ("codeS", 0, 192), ("ms", 0, 192), Op.mult)
-        tt(("f1", 0, 6), ("fc", 0, 6), ("fc", NJ, NJ + 6), Op.max)
-        tt(("f1", 8, 14), ("fc", 2 * NJ, 2 * NJ + 6), ("fc", 3 * NJ, 3 * NJ + 6), Op.max)
-        tt(("FB", 0, 6), ("f1", 0, 6), ("f1", 8, 14), Op.max)
-        cp(("FB", 6, 12), ("B", 0, 6))
-        F, Bb = ("FB", 0, 6), ("B", 0, 6)
+        e = goes.index(0)
+        w0, h0 = 192 * (e // 2), 24 * (e % 2)
+        qe, de, Bb = (src, NB * e, NB * e + 96), ("dd", NB * e, NB * e + 96), ("B", 24 * e, 24 * e + 6)
+        fk = [("fc", NJ * k + h0, NJ * k + h0 + 6) for k in range(4)]
+        ts(("al", 0, 192), ("Aw", w0, w0 + 192), 0.0, Op.is_gt)
+        tt(("ms", 0, 192), ("al", 0, 192), ("hitS", w0, w0 + 192), Op.subtract)
+        tt(("fc", 0, 192), ("codeS", w0, w0 + 192), ("ms", 0, 192), Op.mult)
+        tt(("f1", 0, 6), fk[0], fk[1], Op.max)
+        tt(("f1", 8, 14), fk[2], fk[3], Op.max)
+        F = ("FB", 0, 6)
+        tt(F, ("f1", 0, 6), ("f1", 8, 14), Op.max)
+        cp(("FB", 6, 12), Bb)
         tt(("ed", 0, 6), F, Bb, Op.is_gt)
         ts(("ed", 8, 14), Bb, 0.0, Op.is_gt)
         ts(("cl", 0, 12), ("FB", 0, 12), 4095, Op.bitwise_and)
@@ -591,21 +576,21 @@ def rank_program(g, core, T, topo):
            [full("LB"), ("sb", 8, 14)], [("k0", 0, 96)])
         mm([(("k1", j, 96, 16), LJ("LB", j), ("sb", 0, 6), True, True) for j in range(16)],
            [full("LB"), ("sb", 0, 6)], [("k1", 0, 96)])
-        mm([(("h1", 0, 96), M("CA"), ("dd", 0, 96), True, False), (("h1", 0, 96), M("CA"), (src, 0, 96), False, True)],
-           [M("CA"), ("dd", 0, 96), (src, 0, 96)], [("h1", 0, 96)])
+        mm([(("h1", 0, 96), M("CA"), de, True, False), (("h1", 0, 96), M("CA"), qe, False, True)],
+           [M("CA"), de, qe], [("h1", 0, 96)])
         for x in range(12):
             J = x % 6
             act(("LK", 96 * x, 96 * x + 96), ("LM", 96 * J, 96 * J + 96), Fn.Copy, bias=-1.0, scale=("key1", x, x + 1))
         act(("mf", 0, 96), ("k1", 0, 96), Fn.Copy)
         ts(("mk1", 0, 96), ("k0", 0, 96), KK, Op.is_equal)
         tt(("cm", 0, 96), ("h1", 0, 96), ("mk1", 0, 96), Op.mult)
-        mm([(("k0", 0, 96), M("ISY"), (src, 0, 96), True, False), (("k0", 0, 96), M("RS"), ("cm", 0, 96), False, True)],
-           [M("ISY"), M("RS"), (src, 0, 96), ("cm", 0, 96)], [("k0", 0, 96)])
+        mm([(("k0", 0, 96), M("ISY"), qe, True, False), (("k0", 0, 96), M("RS"), ("cm", 0, 96), False, True)],
+           [M("ISY"), M("RS"), qe, ("cm", 0, 96)], [("k0", 0, 96)])
         for x in range(12):
             w = x // 6
-            e = ("EQ", 96 * x, 96 * x + 96)
-            tt(e, ("LK", 96 * x, 96 * x + 96), ("h0", 96 * w, 96 * w + 96), Op.is_equal)
-            act(e, e, Fn.Copy, accum=("CNT", x, x + 1))
+            eq = ("EQ", 96 * x, 96 * x + 96)
+            tt(eq, ("LK", 96 * x, 96 * x + 96), ("h0", 96 * w, 96 * w + 96), Op.is_equal)
+            act(eq, eq, Fn.Copy, accum=("CNT", x, x + 1))
         cp(("Eb", 0, 96), ("k0", 0, 96))
         ts(("w1", 12, 24), ("CNT", 0, 12), 0.0, Op.is_equal)
         tt(("w1", 24, 36), ("cl", 0, 12), ("DU", 0, 12), Op.subtract)
@@ -614,29 +599,34 @@ def rank_program(g, core, T, topo):
         tt(("w1", 12, 24), ("w1", 48, 60), ("DU", 0, 12), Op.add)
         cp(("OE", 0, 12), ("w1", 12, 24))
         oF, oB, full_w = ("OE", 0, 6), ("OE", 6, 12), ("mkT", 0, MKW)
-        emit("v", lambda: g.vector.tensor_copy(win(oF, MKW), ap(("Eb", 0, 96))), [oF, ("Eb", 0, 96)], [full_w])
-        emit("v", lambda: g.vector.tensor_copy(ap(("vb", 0, 96)), win(oB, MKW)), [oB, full_w], [("vb", 0, 96)])
+        emit("v", lambda: g.vector.tensor_copy(win(oF, MKW), ap(("Eb", 0, 96))), [oF, ("Eb", 0, 96)], [full_w], cost=0.35)
+        emit("v", lambda: g.vector.tensor_copy(ap(("vb", 0, 96)), win(oB, MKW)), [oB, full_w], [("vb", 0, 96)], cost=0.2)
         mm([(("h1", 0, 96), M("ISY"), ("vb", 0, 96), True, False), (("h1", 0, 96), M("DN"), ("vb", 0, 96), False, False),
             (("h1", 0, 96), M("R12"), ("mf", 0, 96), False, True)],
            [M("ISY"), M("DN"), M("R12"), ("vb", 0, 96), ("mf", 0, 96)], [("h1", 0, 96)])
         cp(("Sb", 0, 96), ("h1", 0, 96))
-        emit("v", lambda: g.vector.tensor_copy(win(oB, MKW), ap(("Sb", 0, 96))), [oB, ("Sb", 0, 96)], [full_w])
+        emit("v", lambda: g.vector.tensor_copy(win(oB, MKW), ap(("Sb", 0, 96))), [oB, ("Sb", 0, 96)], [full_w], cost=0.35)
 
-    search("qN", True)
-    close("qN", lambda x, y: "qB" if x // NB == rank else "qA", send)
+    consts_search()
+    search("qN")
+    close("qN", lambda p: "qB" if goes[p] == rank else "qA", send)
     consts_edits()
     edits("qN")
     arrivals()
-    search("qB", False)
+    search("qB")
 
-    def out(c):
-        b = chunk("qF", c)
-        emit("s", lambda: g.sync.dma_start(T.yq[:, c * CH:c * CH + CH], ap(b)), [b], [], "dy%d" % c)
+    def out(p):
+        b, x = ("qF", NB * p, NB * p + NB), NB * came[p]
+        emit("s", lambda: g.sync.dma_start(T.yq[:, x:x + NB], ap(b)), [b], [], "dy%d" % p, 2.5)
 
-    close("qB", lambda x, y: "qF", out)
-    ts(("y1", 0, 96), ("B", 0, 96), 0.0, Op.is_gt)
-    ts(("y2", 0, 96), ("Hb", 0, 96), 1.0, Op.add)
-    tt(("y3", 0, 96), ("y1", 0, 96), ("y2", 0, 96), Op.mult)
-    ts(("yS", 0, 96), ("y3", 0, 96), -1.0, Op.add)
-    emit("s", lambda: g.sync.dma_start(T.yb[:], ap(("yS", 0, 96))), [("yS", 0, 96)], [], "dyb")
-    await_all("g", list(total.items()) + [("sent", nsent[0])])
+    for c in range(2):
+        ts(sm("y1", c), sm("B", c), 0.0, Op.is_gt)
+        ts(sm("y0", c), sm("B", c), 4095, Op.bitwise_and)
+        ts(sm("y2", c), sm("y0", c), 1.0, Op.add)
+        tt(sm("y3", c), sm("y1", c), sm("y2", c), Op.mult)
+        ts(sm("yS", c), sm("y3", c), -1.0, Op.add)
+        for p in (2 * c, 2 * c + 1):
+            b, x = ("yS", 24 * p, 24 * p + 24), 24 * came[p]
+            emit("s", lambda b=b, x=x: g.sync.dma_start(T.yb[:, x:x + 24], ap(b)), [b], [], "db%d" % p, 2.5)
+    close("qB", lambda p: "qF", out)
+    issue(place())

from concourse.mybir import AluOpType as Op, ActivationFunctionType as Fn, AxisListType

W, K, NB = 4096, 1536, 384
CH, NJ = 768, 48
MKW = W + 128
LN256 = 5.545177444479562
CYC, PEC, WAKE, SLACK = 0.00083, 0.00042, 0.17, 0.04

_sets = ["LX", "LY", "LN", "LV0", "LV1", "LV2", "LV3", "LB", "BIG"]
_mats = ["JR", "JA", "JP", "BD", "ID", "HI", "NI", "R0", "ISY", "SRC", "CAQ", "CA", "RS", "DN", "R12"]
SCRATCH = {"mkT": ("sbuf", [128, MKW], "bfloat16"), "land": ("sbuf", [128, NB], "bfloat16")}
for _n in ("qN", "qA", "qB", "qF", "zz", "nn", "vv", "dd", "sd"):
    SCRATCH[_n] = ("sbuf", [128, K], "bfloat16")
for _n in ("qj", "zp"):
    SCRATCH[_n] = ("sbuf", [128, K], "float32")
for _n in _sets:
    SCRATCH[_n] = ("sbuf", [128, 2048], "bfloat16")
for _n in _mats:
    SCRATCH[_n] = ("sbuf", [128, 128], "bfloat16")


def _add(dtype, **widths):
    for n, w in widths.items():
        SCRATCH[n] = ("sbuf", [128, w], dtype)


_add("bfloat16", wS=2, Aw=384, tm=288, Lb=96, khb=32, sb=16, cm=96, Eb=96, vb=96, mf=96, Sb=96)
_add("int32", pi=1, ki=1, ci=4, U=288, UA=288, P=96, Wd=96, S=96, H=96, codeS=384, ch=96, B=96, Hb=96, Li=96, y0=96,
     fc=192, f1=32, FB=12, cl=12, key=12, kh=24, si=16)
_add("float32", col=32, E256=16, geo=64, IT=96, LM=576, DU=12, hitS=384, th=96, m97=96, mt=192, y1=96, y2=96, y3=96, yS=96,
     al=192, ms=192, ed=32, ed2=12, nk=12, key1=12, LK=1152, EQ=1152, CNT=12, w1=64, mk1=96)
_add("uint16", OFF=96, OB=96, OE=12)
BANKS = ("g00", "g01", "g10", "g11", "h0", "h1", "k0", "k1")
for _n in BANKS:
    SCRATCH[_n] = ("psum", [128, 512], "float32")
SEMAPHORES = ["sV", "sA", "sP", "sG", "dw", "dq0", "dq1", "dq2", "dq3", "dm0", "dm1", "dy0", "dy1", "dy2", "dy3",
              "db0", "db1", "db2", "db3", "arr0", "arr1", "arr2", "arr3", "sent", "rin", "rls"]


def relay_of(src, dst, cores, topo):
    k = 0
    for d in cores:
        if d == src or topo.may_write(src, d):
            if d == dst:
                return None
            continue
        own = [c for c in topo.cores_of(src) if c != src and topo.may_write(c, d)]
        near = [c for c in own if topo.die(c) == topo.die(src)]
        far = [c for c in own if topo.die(c) != topo.die(src)]
        if d == dst:
            return near[0] if k % 2 == 0 else far[0]
        k += 1
    return None


def held_order(rank):
    return [(rank + k) % 4 for k in (0, 1, 3, 2)], [(rank - k) % 4 for k in (0, 1, 3, 2)]


def count(mask):
    return bin(mask).count("1")


def off_chip_mask(src, cores, topo):
    for d in cores:
        if d != src and topo.may_write(src, d):
            return topo.mask(src, d)
    return 0


def rank_program(g, core, T, topo):
    cores = list(T.cores)
    rank = T.rank_of(core)
    if rank is None:
        for a in cores:
            for b in cores:
                if a == b or relay_of(a, b, cores, topo) != core:
                    continue
                r = T.rank_of(a)
                m_in = off_chip_mask(a, cores, topo) & topo.mask(a, core)
                m_out = topo.mask(core, b)
                rid, pid = topo.addr(b, core)
                p = NB * held_order(T.rank_of(b))[1].index(r)
                g.wait_ge(T.sem.rin, count(m_in))
                g.remote_dma(T.qB[:, p:p + NB], T.land[:], T.sem["arr%d" % r], T.sem.rls, pid, rid, m_out)
                g.wait_ge(T.sem.rls, count(m_out))
        return

    Q = {"v": g.vector, "a": g.scalar, "p": g.tensor, "g": g, "s": g.sync}
    SEM = {"v": "sV", "a": "sA", "p": "sP", "g": "sG"}
    ops = []
    rec = {}

    def emit(q, fn, reads, writes, sem=None, cost=0.1, ev=None, after=()):
        i = len(ops)
        waits, order = set(after), set()
        for kind, lst in (("r", reads), ("w", writes)):
            for b in lst:
                nm, lo, hi = b[0], b[1], b[2]
                r = rec.setdefault(nm, [])
                if nm in BANKS:
                    for x in r:
                        if x[3] == i:
                            continue
                        if x[2] != q or (x[4] == "w" and q != "p"):
                            waits.add(x[3])
                        else:
                            order.add(x[3])
                    r[:] = [x for x in r if x[2] == q or x[3] == i]
                else:
                    for x in r:
                        if x[3] != i and x[0] < hi and lo < x[1] and (kind == "w" or x[4] == "w"):
                            waits.add(x[3])
                    if kind == "w":
                        r[:] = [x for x in r if not (lo <= x[0] and x[1] <= hi)]
                r.append((lo, hi, q, i, kind))
        ops.append((q, fn, sem, cost, waits, order - waits, ev))
        return i

    def place():
        n = len(ops)
        succ = [[] for _ in ops]
        need = [0] * n
        for i in range(n):
            for d in ops[i][4] | ops[i][5]:
                succ[d].append(i)
                need[i] += 1
        prio = [0.0] * n
        for i in reversed(range(n)):
            prio[i] = ops[i][3] + max([prio[j] + (WAKE if i in ops[j][4] else 0.0) for j in succ[i]] + [0.0])
        at = [0.0] * n
        ready = [i for i in range(n) if need[i] == 0]
        free = {}
        seq = []
        while ready:
            st = [max(free.get(ops[i][0], 0.0), at[i]) for i in ready]
            t = min(st)
            q = ops[ready[st.index(t)]][0]
            i = -max((prio[i], -i) for i, x in zip(ready, st) if ops[i][0] == q and x <= t + SLACK)[1]
            t = max(free.get(q, 0.0), at[i])
            ready.remove(i)
            seq.append(i)
            end = t + ops[i][3]
            free[q] = t + 0.05 if ops[i][2] is not None else end
            for j in succ[i]:
                at[j] = max(at[j], end + WAKE if i in ops[j][4] else t)
                need[j] -= 1
                if need[j] == 0:
                    ready.append(j)
        return seq

    def issue(seq):
        cnt = {"v": 0, "a": 0, "p": 0, "g": 0}
        clock = {q: {} for q in Q}
        clkat, evs, total = {}, {}, {}

        def see(q, ev):
            c = clock[q]
            for s, x in list(clkat.get(ev, {}).items()) + [ev]:
                if c.get(s, 0) < x:
                    c[s] = x

        def await_all(q, want):
            best = {}
            for s, x in want:
                best[s] = max(best.get(s, 0), x)
            todo = [(s, x) for s, x in best.items() if clock[q].get(s, 0) < x]
            for e in [e for e in todo if not any(o != e and clkat.get(o, {}).get(e[0], 0) >= e[1] for o in todo)]:
                Q[q].wait_ge(T.sem[e[0]], e[1])
                see(q, e)

        for i in seq:
            q, fn, sem, cost, waits, order, ev = ops[i]
            if fn is None:
                evs[i] = ev
                clkat[ev] = {}
                total[ev[0]] = ev[1]
                continue
            await_all(q, [evs[d] for d in waits if evs.get(d) is not None])
            ins = fn()
            if ev is not None:
                total[ev[0]] = total.get(ev[0], 0) + ev[1]
                continue
            if sem is None:
                cnt[q] += 1
                evs[i] = (SEM[q], cnt[q])
                ins.then_inc(T.sem[SEM[q]], 1)
            else:
                evs[i] = (sem, 16)
                ins.then_inc(T.sem[sem], 16)
            total[evs[i][0]] = evs[i][1]
            c = dict(clock[q])
            c[evs[i][0]] = evs[i][1]
            clkat[evs[i]] = c
        await_all("g", list(total.items()))

    def wide(b):
        return (b[2] - b[1] + (b[3] - 1 if len(b) > 3 else 0)) // (b[3] if len(b) > 3 else 1)

    def cost(out, ins, two=False):
        n = wide(out)
        if two:
            n *= 1 if any(b[0] in BANKS for b in ins) else 2
        elif all(SCRATCH[b[0]][2] in ("bfloat16", "uint16") for b in [out] + ins):
            n /= 2
        return max(64, n) * CYC + 0.03

    def ap(b):
        if len(b) > 3:
            return T[b[0]][:, b[1]:b[2]:b[3]]
        return T[b[0]][:, b[1]:b[2]]

    def isap(x):
        return isinstance(x, tuple)

    def tt(out, a, b, op):
        return emit("v", lambda: g.vector.tensor_tensor(ap(out), ap(a), ap(b), op), [a, b], [out], cost=cost(out, [a, b], True))

    def ts(out, a, s1, op0, s2=None, op1=None):
        rd = [a] + [s for s in (s1, s2) if isap(s)]
        x1 = ap(s1) if isap(s1) else s1
        x2 = ap(s2) if isap(s2) else s2
        if op1 is None:
            return emit("v", lambda: g.vector.tensor_scalar(ap(out), ap(a), x1, None, op0), rd, [out], cost=cost(out, [a]))
        return emit("v", lambda: g.vector.tensor_scalar(ap(out), ap(a), x1, x2, op0, op1), rd, [out], cost=cost(out, [a]))

    def cp(out, a):
        return emit("v", lambda: g.vector.tensor_copy(ap(out), ap(a)), [a], [out], cost=cost(out, [a]))

    def fill(out, x):
        return emit("v", lambda: g.vector.memset(ap(out), x), [], [out])

    def act(out, a, fn, bias=0.0, scale=1.0, accum=None):
        rd = [a] + [s for s in (bias, scale) if isap(s)]
        kw = {}
        if isap(bias) or bias != 0.0:
            kw["bias"] = ap(bias) if isap(bias) else bias
        if isap(scale) or scale != 1.0:
            kw["scale"] = ap(scale) if isap(scale) else scale
        wr = [out]
        if accum is not None:
            kw["accum_out"] = ap(accum)
            wr = [out, accum]
        return emit("a", lambda: g.scalar.activation(ap(out), ap(a), fn, **kw), rd, wr, cost=wide(out) * CYC + 0.05)

    def mm(seq, reads, writes):
        def go():
            ins = None
            for o, l, r, st, sp in seq:
                ins = g.tensor.matmul(ap(o), ap(l), ap(r), st, sp)
            return ins
        return emit("p", go, reads, writes, cost=sum(max(64, wide(o)) for o, l, r, st, sp in seq) * PEC + 0.03)

    def LJ(nm, j):
        return (nm, 128 * j, 128 * j + 128)

    def M(nm):
        return (nm, 0, 128)

    def full(nm):
        return (nm, 0, 2048)

    def word(nm, out, src, base, w, extra=None, strided=True):
        seq = []
        if extra is not None:
            seq.append((out, extra[0], extra[1], True, False))
        for j in range(16):
            r = (src, base + j, base + 16 * w, 16) if strided else (src, base + w * j, base + w * (j + 1))
            seq.append((out, LJ(nm, j), r, extra is None and j == 0, j == 15))
        rd = [full(nm), (src, base, base + 16 * w)]
        if extra is not None:
            rd += [extra[0], extra[1]]
        return mm(seq, rd, [out])

    goes, came = held_order(rank)
    emit("a", lambda: g.scalar.dma_start(ap(("wS", 0, 2)), T.wt[:]), [], [("wS", 0, 2)], "dw", 2.0)
    for p in range(4):
        b = ("qN", NB * p, NB * p + NB)
        emit("s", lambda b=b, x=NB * goes[p]: g.sync.dma_start(ap(b), T.qs[:, x:x + NB]), [], [b], "dq%d" % p, 2.5 + 0.5 * p)
    emit("a", lambda: g.scalar.dma_start(ap(("mkT", 0, 2048)), T.mk[:, 0:2048]), [], [("mkT", 0, 2048)], "dm0", 7.0)
    emit("s", lambda: g.sync.dma_start(ap(("mkT", 2048, W)), T.mk[:, 2048:W]), [], [("mkT", 2048, W)], "dm1", 7.0)

    def C(i):
        return ("col", i, i + 1)
    KC, PB, NBI, LBI, WN, KP1, RCOL, KK, T0, T1, R120 = [C(i) for i in range(11)]
    RC = [C(12 + r) for r in range(4)]
    KJ = [C(16 + J) for J in range(6)]
    KLT = C(22)
    T2, T3, T4, T5 = [C(24 + i) for i in range(4)]

    def iota(out, pattern, base, cm, flag=True):
        if flag:
            return emit("g", lambda: g.iota(ap(out), pattern, base, cm, allow_small_or_imprecise_dtypes=True), [], [out])
        return emit("g", lambda: g.iota(ap(out), pattern, base, cm), [], [out])

    def pick(out, a, pattern, op, x, base, cm):
        return emit("g", lambda: g.affine_select(ap(out), ap(a), pattern, op, x, base, cm), [a], [out],
                    cost=0.17 + 2 * wide(out) * CYC)

    iota(("pi", 0, 1), [[0, 1]], 0, 1, False)
    iota(M("JR"), [[0, 8], [1, 16]], 0, 0)
    pick(M("JA"), M("JR"), [[-16, 8], [0, 16]], Op.is_ge, 99.0, 0, 1)
    pick(M("JP"), M("JA"), [[16, 8], [0, 16]], Op.is_ge, 99.0, 15, -1)
    ts(("ki", 0, 1), ("pi", 0, 1), 15, Op.bitwise_and)
    cp(KC, ("ki", 0, 1))
    ts(PB, KC, 256.0, Op.mult)
    ts(NBI, KC, -256.0, Op.mult)
    for r in range(4):
        ts(RC[r], KC, float(12 + r), Op.is_equal)
    ts(M("ID"), M("JP"), KC, Op.is_equal)
    ts(M("BD"), M("JP"), 15.5, Op.is_le)
    ts(M("R0"), M("BD"), RC[0], Op.mult, 256.0, Op.mult)
    for j in range(16):
        ts(LJ("BIG", j), M("JP"), float(j), Op.is_equal)
    ts(full("LX"), full("BIG"), ("wS", 0, 1), Op.mult)
    ts(full("LY"), full("BIG"), ("wS", 1, 2), Op.mult)
    act(full("LV0"), full("BIG"), Fn.Copy, scale=RC[0])
    for r in (1, 2):
        pick(full("LV%d" % r), full("BIG"), [[0, 16], [-16, 8], [0, 16]], Op.is_equal, 0.0, -12 - r, 1)
    iota(M("SRC"), [[0, 8], [1, 4], [1, 4]], 13, 0)
    iota(("IT", 0, 96), [[1, 96]], 0, 0)
    iota(("w1", 0, 12), [[0, 2], [16, 6]], W, 0)

    def consts_search():
        ts(("E256", 0, 16), ("JR", 0, 16), KC, Op.is_equal, 256.0, Op.mult)
        fill(("geo", 0, 16), 1.0 / 256)
        fill(("geo", 16, 32), 0.0)
        emit("v", lambda: g.vector.tensor_tensor_scan(ap(("geo", 32, 48)), ap(("geo", 0, 16)), ap(("geo", 16, 32)), -128.0,
                                                      Op.mult, Op.add), [("geo", 0, 32)], [("geo", 32, 48)])
        tt(("geo", 48, 60), ("geo", 32, 44), ("E256", 0, 12), Op.mult)
        emit("v", lambda: g.vector.tensor_reduce(ap(WN), ap(("geo", 48, 60)), AxisListType.X, Op.add), [("geo", 48, 60)], [WN])
        ts(full("LN"), full("BIG"), WN, Op.mult, 1.0 / 256, Op.mult)
        ts(full("LV3"), full("BIG"), RC[3], Op.mult)
        ts(M("NI"), M("ID"), -1.0, Op.mult)
        for j in range(16):
            ts(LJ("LB", j), M("BD"), ("E256", j, j + 1), Op.mult)
        ts(M("HI"), M("ID"), 0.5, Op.mult)
        ts(T0, KC, 11.5, Op.is_gt, -100000.0, Op.mult)
        ts(T1, NBI, 128.0, Op.subtract)
        tt(LBI, T0, T1, Op.add)
        fill(("mkT", W, MKW), 0.0)

    def consts_edits():
        ts(KLT, KC, 11.5, Op.is_lt)
        ts(M("ISY"), M("ID"), KLT, Op.mult)
        ts(M("CAQ"), M("SRC"), KC, Op.is_equal)
        tt(M("CA"), M("CAQ"), M("BD"), Op.mult)
        ts(("ci", 0, 1), ("ki", 0, 1), 3, Op.bitwise_and)
        ts(T2, KC, 11.5, Op.is_gt, 50.0, Op.mult)
        ts(T3, ("ci", 0, 1), 12.0, Op.add)
        tt(RCOL, T2, T3, Op.add)
        ts(M("RS"), M("JP"), RCOL, Op.is_equal)
        ts(("ci", 1, 2), ("ki", 0, 1), 2, Op.arith_shift_right)
        ts(KK, ("ci", 1, 2), -256.0, Op.mult, 768.0, Op.add)
        ts(T4, KC, 11.5, Op.is_lt, 50.0, Op.mult)
        ts(T5, KC, 1.0, Op.add)
        tt(KP1, T4, T5, Op.add)
        ts(M("DN"), M("JP"), KP1, Op.is_equal)
        ts(R120, RC[0], 1.0 / 256, Op.mult)
        ts(M("R12"), M("ID"), R120, Op.mult)
        ts(("DU", 0, 12), ("w1", 0, 12), KC, Op.add)
        for J in range(6):
            ts(KJ[J], KC, 16.0 * J, Op.add)
            ts(("LM", 96 * J, 96 * J + 96), ("IT", 0, 96), KJ[J], Op.is_lt)

    def sm(nm, c, k=0, n=1):
        lo = c * NJ * n + k * NJ
        return (nm, lo, lo + NJ)

    def half(nm, c, h):
        lo = c * CH + h * NB
        return (nm, lo, lo + NB)

    def chunk(nm, c):
        return (nm, c * CH, c * CH + CH)

    def gb(c, h):
        return "g%d%d" % (c, h)

    def jmajor(c, src):
        for h, bk in ((0, "h%d" % c), (1, "k%d" % c)):
            seq = []
            for x in range(8):
                seq.append(((bk, x * NJ, x * NJ + NJ), M("ID"), (src, c * CH + 8 * h + x, c * CH + CH, 16), True, True))
            mm(seq, [M("ID"), chunk(src, c)], [(bk, 0, NB)])
            act(half("qj", c, h), (bk, 0, NB), Fn.Identity, bias=PB)

    def lengths(c, src, rs):
        for r in rs:
            word("LV%d" % r, ("k%d" % c, r * NJ, r * NJ + NJ), src, c * CH, NJ)
        lo, hi = rs[0] * NJ, rs[-1] * NJ + NJ
        act(("Aw", c * 192 + lo, c * 192 + hi), ("k%d" % c, lo, hi), Fn.Copy)

    def P1(c, s, src):
        m = sm("Aw", c, s - 1, 4)
        for h in range(2):
            seq = []
            for x in range(8):
                j = 8 * h + x
                o = (gb(c, h), x * NJ, x * NJ + NJ)
                if s == 1:
                    seq.append((o, M("R0"), (src, c * CH + j, c * CH + CH, 16), True, True))
                else:
                    seq.append((o, LJ("LB", j), m, True, True))
            mm(seq, [M("R0"), chunk(src, c)] if s == 1 else [full("LB"), m], [(gb(c, h), 0, NB)])

    def V1(c):
        for h in range(2):
            tt(half("zp", c, h), half("qj", c, h), (gb(c, h), 0, NB), Op.min)

    def A1(c):
        for h in range(2):
            act(half("zz", c, h), half("zp", c, h), Fn.Relu, bias=NBI)

    def A2(c, s):
        m = sm("Aw", c, s - 1, 4)
        act(sm("m97", c), m, Fn.Copy, scale=97.0)
        act(sm("th", c), m, Fn.Silu, scale=-LN256)
        act(sm("mt", c, s % 2, 2), m, Fn.Copy, bias=8192.0 + 65536.0 * s, scale=4096.0)

    def P2(c):
        word("LX", ("h%d" % c, 0, NJ), "zz", c * CH, NJ, strided=False)
        word("LY", ("h%d" % c, NJ, 2 * NJ), "zz", c * CH, NJ, strided=False)

    def V2(c):
        hb, o = "h%d" % c, c * 3 * NJ
        cp(("U", o, o + 2 * NJ), (hb, 0, 2 * NJ))
        tt(sm("U", c, 2, 3), (hb, NJ, 2 * NJ), sm("m97", c), Op.add)
        ts(("UA", o, o + 3 * NJ), ("U", o, o + 3 * NJ), 4095, Op.bitwise_and)
        tt(sm("P", c), sm("UA", c, 0, 3), sm("UA", c, 1, 3), Op.mult)
        ts(sm("Wd", c), sm("UA", c, 2, 3), 32.0, Op.mult, -131072.0, Op.add)
        tt(sm("S", c), sm("P", c), sm("Wd", c), Op.add)
        ts(sm("H", c), sm("S", c), 5, Op.arith_shift_right, 4095, Op.bitwise_and)
        cp(sm("OFF", c), sm("H", c))

    def win(off, w=W):
        return T.mkT[:, 0:w].indirect(ap(off))

    def gathered(o, off, q, op):
        emit("v", lambda: g.vector.tensor_tensor(ap(o), win(off), ap(q), op), [("mkT", 0, W), off, q], [o],
             cost=0.08 + 1.5 * CYC * wide(o))

    def A3(c):
        o, off = chunk("vv", c), sm("OFF", c)
        emit("a", lambda: g.scalar.activation(ap(o), win(off), Fn.Copy), [("mkT", 0, W), off], [o],
             cost=0.1 + 1.5 * CYC * wide(o))

    def held(c, w):
        return ("k%d" % c, NJ, 2 * NJ) if w == 0 else ("h%d" % c, (w - 1) * NJ, w * NJ)

    def P4(c, s):
        for w in range(4 - s):
            word("LV%d" % w, held(c, w), "vv", c * CH, NJ, extra=(M("NI"), sm("Aw", c, s + w, 4)))

    def V4(c, s):
        hit, code = sm("hitS", c, s - 1, 4), sm("codeS", c, s - 1, 4)
        tt(code, sm("H", c), sm("mt", c, s % 2, 2), Op.add)
        tt(hit, ("k%d" % c, 0, NJ), sm("th", c), Op.is_gt)
        for w in range(4 - s):
            t = ("tm", c * 144 + w * NJ, c * 144 + w * NJ + NJ)
            tt(t, held(c, w), hit, Op.mult)
            tt(sm("Aw", c, s + w, 4), sm("Aw", c, s + w, 4), t, Op.add)
        tt(sm("B" if s == 1 else "ch", c), code, hit, Op.mult)
        if s > 1:
            tt(sm("B", c), sm("B", c), sm("ch", c), Op.max)

    def La(c, src):
        ts(sm("Li", c), sm("B", c), 12, Op.arith_shift_right, 15, Op.bitwise_and)
        ts(sm("Hb", c), sm("B", c), 4095, Op.bitwise_and)
        cp(sm("Lb", c), sm("Li", c))
        cp(sm("OB", c), sm("Hb", c))
        for h in range(2):
            r = ("Lb", c * NJ + 24 * h, c * NJ + 24 * h + 24)
            bk = (gb(c, h), 0, NB)
            mm([((gb(c, h), j, NB, 16), LJ("LB", j), r, True, True) for j in range(16)], [full("LB"), r], [bk])
            act(bk, bk, Fn.Sign, bias=LBI)
            gathered(half("dd", c, h), ("OB", c * NJ + 24 * h, c * NJ + 24 * h + 24), half(src, c, h), Op.subtract)

    def Lb(c, h, src, to):
        bk, d, sd, q = (gb(c, h), 0, NB), half("dd", c, h), half("sd", c, h), half(src, c, h)
        tt(sd, d, bk, Op.mult)
        mm([(bk, M("ID"), q, True, False), (bk, M("HI"), d, False, False), (bk, M("HI"), sd, False, True)],
           [M("ID"), M("HI"), q, d, sd], [bk])
        act(half(to, c, h), bk, Fn.Copy)

    def search(src):
        for s in range(1, 5):
            for c in range(2):
                if s == 1:
                    jmajor(c, src)
                P1(c, s, src)
                if s == 1:
                    lengths(c, src, [0])
                A2(c, s)
                V1(c)
                A1(c)
                P2(c)
                if s == 1:
                    lengths(c, src, [1, 2, 3])
                V2(c)
                gathered(chunk("nn", c), sm("OFF", c), chunk(src, c), Op.not_equal)
                if s < 4:
                    A3(c)
                word("LN", ("k%d" % c, 0, NJ), "nn", c * CH, NJ)
                P4(c, s)
                V4(c, s)

    def close(src, dest, after):
        for c in range(2):
            La(c, src)
            for h in range(2):
                Lb(c, h, src, dest(2 * c + h))
                after(2 * c + h)

    omask = off_chip_mask(core, cores, topo)
    sends = []

    def send(p):
        s = goes[p]
        if s == rank:
            return
        b = ("qA", NB * p, NB * p + NB)
        rel = relay_of(core, cores[s], cores, topo)
        to = cores[s] if rel is None else rel
        m = omask & topo.mask(core, to)
        rid, pid = topo.addr(to, core)
        x = NB * held_order(s)[1].index(rank)
        dst, sem = (T.land[:], "rin") if rel is not None else (T.qB[:, x:x + NB], "arr%d" % rank)
        sends.append(emit("g", lambda: g.remote_dma(dst, ap(b), T.sem[sem], T.sem.sent, pid, rid, m), [b], [], None, 0.3,
                          ("sent", count(m))))

    def arrivals():
        for p in range(4):
            s = came[p]
            if s != rank:
                rel = relay_of(cores[s], core, cores, topo)
                n = count(topo.mask(cores[s] if rel is None else rel, core))
                emit("x%d" % s, None, [], [("qB", NB * p, NB * p + NB)], None, 4.0 if rel is None else 8.0, ("arr%d" % s, n),
                     sends[:1] if p < 2 else sends)

    def edits(src):
        e = goes.index(0)
        w0, h0 = 192 * (e // 2), 24 * (e % 2)
        qe, de, Bb = (src, NB * e, NB * e + 96), ("dd", NB * e, NB * e + 96), ("B", 24 * e, 24 * e + 6)
        fk = [("fc", NJ * k + h0, NJ * k + h0 + 6) for k in range(4)]
        ts(("al", 0, 192), ("Aw", w0, w0 + 192), 0.0, Op.is_gt)
        tt(("ms", 0, 192), ("al", 0, 192), ("hitS", w0, w0 + 192), Op.subtract)
        tt(("fc", 0, 192), ("codeS", w0, w0 + 192), ("ms", 0, 192), Op.mult)
        tt(("f1", 0, 6), fk[0], fk[1], Op.max)
        tt(("f1", 8, 14), fk[2], fk[3], Op.max)
        F = ("FB", 0, 6)
        tt(F, ("f1", 0, 6), ("f1", 8, 14), Op.max)
        cp(("FB", 6, 12), Bb)
        tt(("ed", 0, 6), F, Bb, Op.is_gt)
        ts(("ed", 8, 14), Bb, 0.0, Op.is_gt)
        ts(("cl", 0, 12), ("FB", 0, 12), 4095, Op.bitwise_and)
        ts(("si", 0, 6), F, 12, Op.arith_shift_right, 15, Op.bitwise_and)
        ts(("si", 8, 14), Bb, 16, Op.arith_shift_right)
        for o in (0, 6):
            tt(("ed2", o, o + 6), ("ed", 0, 6), ("ed", 8, 14), Op.mult)
        ts(("nk", 0, 12), ("ed2", 0, 12), -8192.0, Op.mult, 8192.0, Op.add)
        tt(("key", 0, 12), ("cl", 0, 12), ("nk", 0, 12), Op.add)
        ts(("key1", 0, 12), ("key", 0, 12), 1.0, Op.add)
        ts(("kh", 0, 12), ("key", 0, 12), 6, Op.arith_shift_right)
        ts(("kh", 12, 24), ("key", 0, 12), 63, Op.bitwise_and)
        ts(("khb", 0, 12), ("kh", 0, 12), 0.25, Op.mult)
        ts(("khb", 16, 28), ("kh", 12, 24), 1.0 / 256, Op.mult)
        ts(("sb", 0, 6), ("si", 0, 6), -2.0, Op.add)
        cp(("sb", 8, 14), ("si", 8, 14))
        seq = []
        for j in range(16):
            o = ("h0", j, 192, 16)
            seq += [(o, LJ("LB", j), ("khb", 0, 12), True, False), (o, LJ("LB", j), ("khb", 16, 28), False, True)]
        mm(seq, [full("LB"), ("khb", 0, 12), ("khb", 16, 28)], [("h0", 0, 192)])
        mm([(("k0", j, 96, 16), LJ("LB", j), ("sb", 8, 14), True, True) for j in range(16)],
           [full("LB"), ("sb", 8, 14)], [("k0", 0, 96)])
        mm([(("k1", j, 96, 16), LJ("LB", j), ("sb", 0, 6), True, True) for j in range(16)],
           [full("LB"), ("sb", 0, 6)], [("k1", 0, 96)])
        mm([(("h1", 0, 96), M("CA"), de, True, False), (("h1", 0, 96), M("CA"), qe, False, True)],
           [M("CA"), de, qe], [("h1", 0, 96)])
        for x in range(12):
            J = x % 6
            act(("LK", 96 * x, 96 * x + 96), ("LM", 96 * J, 96 * J + 96), Fn.Copy, bias=-1.0, scale=("key1", x, x + 1))
        act(("mf", 0, 96), ("k1", 0, 96), Fn.Copy)
        ts(("mk1", 0, 96), ("k0", 0, 96), KK, Op.is_equal)
        tt(("cm", 0, 96), ("h1", 0, 96), ("mk1", 0, 96), Op.mult)
        mm([(("k0", 0, 96), M("ISY"), qe, True, False), (("k0", 0, 96), M("RS"), ("cm", 0, 96), False, True)],
           [M("ISY"), M("RS"), qe, ("cm", 0, 96)], [("k0", 0, 96)])
        for x in range(12):
            w = x // 6
            eq = ("EQ", 96 * x, 96 * x + 96)
            tt(eq, ("LK", 96 * x, 96 * x + 96), ("h0", 96 * w, 96 * w + 96), Op.is_equal)
            act(eq, eq, Fn.Copy, accum=("CNT", x, x + 1))
        cp(("Eb", 0, 96), ("k0", 0, 96))
        ts(("w1", 12, 24), ("CNT", 0, 12), 0.0, Op.is_equal)
        tt(("w1", 24, 36), ("cl", 0, 12), ("DU", 0, 12), Op.subtract)
        tt(("w1", 36, 48), ("w1", 12, 24), ("ed2", 0, 12), Op.mult)
        tt(("w1", 48, 60), ("w1", 24, 36), ("w1", 36, 48), Op.mult)
        tt(("w1", 12, 24), ("w1", 48, 60), ("DU", 0, 12), Op.add)
        cp(("OE", 0, 12), ("w1", 12, 24))
        oF, oB, full_w = ("OE", 0, 6), ("OE", 6, 12), ("mkT", 0, MKW)
        emit("v", lambda: g.vector.tensor_copy(win(oF, MKW), ap(("Eb", 0, 96))), [oF, ("Eb", 0, 96)], [full_w], cost=0.35)
        emit("v", lambda: g.vector.tensor_copy(ap(("vb", 0, 96)), win(oB, MKW)), [oB, full_w], [("vb", 0, 96)], cost=0.2)
        mm([(("h1", 0, 96), M("ISY"), ("vb", 0, 96), True, False), (("h1", 0, 96), M("DN"), ("vb", 0, 96), False, False),
            (("h1", 0, 96), M("R12"), ("mf", 0, 96), False, True)],
           [M("ISY"), M("DN"), M("R12"), ("vb", 0, 96), ("mf", 0, 96)], [("h1", 0, 96)])
        cp(("Sb", 0, 96), ("h1", 0, 96))
        emit("v", lambda: g.vector.tensor_copy(win(oB, MKW), ap(("Sb", 0, 96))), [oB, ("Sb", 0, 96)], [full_w], cost=0.35)

    consts_search()
    search("qN")
    close("qN", lambda p: "qB" if goes[p] == rank else "qA", send)
    consts_edits()
    edits("qN")
    arrivals()
    search("qB")

    def out(p):
        b, x = ("qF", NB * p, NB * p + NB), NB * came[p]
        emit("s", lambda: g.sync.dma_start(T.yq[:, x:x + NB], ap(b)), [b], [], "dy%d" % p, 2.5)

    for c in range(2):
        ts(sm("y1", c), sm("B", c), 0.0, Op.is_gt)
        ts(sm("y0", c), sm("B", c), 4095, Op.bitwise_and)
        ts(sm("y2", c), sm("y0", c), 1.0, Op.add)
        tt(sm("y3", c), sm("y1", c), sm("y2", c), Op.mult)
        ts(sm("yS", c), sm("y3", c), -1.0, Op.add)
        for p in (2 * c, 2 * c + 1):
            b, x = ("yS", 24 * p, 24 * p + 24), 24 * came[p]
            emit("s", lambda b=b, x=x: g.sync.dma_start(T.yb[:, x:x + 24], ap(b)), [b], [], "db%d" % p, 2.5)
    close("qB", lambda p: "qF", out)
    issue(place())
